import numpy as np
import ml_dtypes


def mxq(x, axis, fmt="e4m3"):
    dtype, down = {"e4m3": (ml_dtypes.float8_e4m3fn, 7), "e5m2": (ml_dtypes.float8_e5m2, 14)}[fmt]
    v = np.moveaxis(np.asarray(x, np.float32).astype(ml_dtypes.bfloat16).astype(np.float64), axis, -1)
    blocks = v.reshape(v.shape[:-1] + (-1, 32))
    amax = np.abs(blocks).max(-1, keepdims=True)
    byte = np.maximum(np.where(amax > 0, np.frexp(amax)[1] - 1 + 127, 0) - down, 1)
    scale = np.exp2(byte - 127.0)
    codes = (blocks / scale).astype(np.float32).astype(dtype).astype(np.float64)
    return np.moveaxis((codes * scale).reshape(v.shape), -1, axis)


WIDE = False


def mx_kscale(k):
    if not WIDE:
        return np.ones(k)
    levels = np.array([10, -10, 5, -5, 0])
    if k % 512:
        return np.exp2(np.random.permutation(np.resize(levels, k // 32))).repeat(32)
    a = np.empty((k // 512, 16))
    for p in range(k // 512):
        a[p, :8] = np.random.permutation(np.resize(levels, 8))
        for g in range(8):
            far = levels[np.abs(levels - a[p, g]) >= 10]
            a[p, g + 8] = far[np.random.randint(len(far))]
    return np.exp2(a.ravel()).repeat(32)


def f64(x):
    return np.asarray(x).astype(np.float64)


def striped(idx):
    return np.tile(idx.reshape(-1, 16).T, (8, 1)).astype(np.uint16)


def unstriped(offs):
    return offs[:16].T.reshape(-1).astype(np.int64)


def pack_weight(w):
    k, n = w.shape
    w = f64(np.asarray(w, np.float32).astype(ml_dtypes.bfloat16)).reshape(k // 32, 32, n)
    amax = np.abs(w).max(1)
    byte = np.clip(np.where(amax > 0, np.frexp(amax)[1] - 1 + 127 - 7, 1), 1, 254)
    scaled = (w * np.exp2(127.0 - byte)[:, None, :]).reshape(k, n).astype(np.float32)
    words = np.ascontiguousarray(scaled.reshape(k // 512, 128, 4, n).transpose(0, 1, 3, 2)).astype(ml_dtypes.float8_e4m3fn).view(np.uint8)
    return words, np.ascontiguousarray(byte.astype(np.uint8).reshape(k // 512, 16, n))


def unpack_weight(words, scales):
    g, p, n, _ = words.shape
    vals = np.ascontiguousarray(words).view(ml_dtypes.float8_e4m3fn).astype(np.float64) * np.repeat(np.exp2(scales.astype(np.float64) - 127.0), 8, axis=1)[..., None]
    return vals.transpose(0, 1, 3, 2).reshape(g * 512, n)


def relu(v):
    return np.maximum(v, 0.0)

def planes(y):
    n, m = y.shape
    v = y.astype(np.float32).astype(ml_dtypes.bfloat16).astype(np.float64).reshape(n // 32, 32, m)
    top = np.abs(v).max(1)
    byte = np.clip(np.where(top > 0, np.frexp(top)[1] - 1 + 127 - 7, 1), 1, 254)
    codes = (v * np.exp2(127.0 - byte)[:, None, :]).reshape(n, m).astype(np.float32).astype(ml_dtypes.float8_e4m3fn).view(np.uint8)
    words = codes.reshape(n // 512, 128, 4, m).transpose(0, 1, 3, 2)
    return np.ascontiguousarray(words), np.ascontiguousarray(byte.astype(np.uint8).reshape(n // 512, 16, m))


K, T, S, H = 512, 2048, 512, 512


def setup_inputs():
    n = np.random.standard_normal
    s = mx_kscale(K)[:, None]
    u = mx_kscale(S)
    packed_xT = pack_weight(n((K, T)) * s)
    return {
        "x_words": packed_xT[0],
        "x_scales": packed_xT[1],
        "wa": (n((K, H)) / np.sqrt(K) / s).astype(np.float32),
        "wb": (n((K, H)) / np.sqrt(K) / s).astype(np.float32),
        "gt": (np.random.uniform(0.5, 1.5, (S, 1)) * u[:, None]).astype(np.float32),
        "gi": (np.random.uniform(0.5, 1.5, (S, 1)) / u[:, None]).astype(np.float32),
        "offs": striped(np.random.permutation(T)[:S]),
    }


def reference(x_words, x_scales, wa, wb, gt, gi, offs):
    xq = unpack_weight(x_words, x_scales)[:, unstriped(offs)]
    a = xq.T @ mxq(f64(wa), 0, "e4m3")
    z = f64(gt) * relu(a)
    b = xq.T @ mxq(f64(wb), 0, "e4m3")
    z2 = f64(gi) * b
    out_0 = 0.0625 * ((mxq(z, 0, "e4m3").T @ mxq(z2, 0, "e4m3")))
    return (out_0,) + planes(out_0)

@@ -1,0 +1,233 @@
+from contextlib import ExitStack
+
+import concourse.mybir as mybir
+
+K, T, S, H = 512, 2048, 512, 512
+FLOPS = 3 * 2 * 512 * 512 * 512
+
+F32 = mybir.dt.float32
+BF16 = mybir.dt.bfloat16
+I32 = mybir.dt.int32
+U32 = mybir.dt.uint32
+U16 = mybir.dt.uint16
+U8 = mybir.dt.uint8
+FP8X4 = mybir.dt.float8_e4m3fn_x4
+ALU = mybir.AluOpType
+COPY = mybir.ActivationFunctionType.Copy
+
+P = 128
+PACK = 4
+LEAD = 512
+SCALAR_ROUNDS = 1
+HALF = H // 2
+CHUNK = 128
+CHUNKS = H // CHUNK
+OUT_SCALE = 0.0625
+
+
+def tile_picked_bilpool_relu_po_kernel(
+    tc, x_words, x_scales, wa, wb, gt, gi, offs, out_0, out_1, out_2
+):
+    nc = tc.nc
+    with ExitStack() as ctx:
+        keep = ctx.enter_context(tc.tile_pool(name="keep", bufs=1))
+        ring = ctx.enter_context(tc.tile_pool(name="ring", bufs=2))
+        psum = ctx.enter_context(tc.psum_pool(name="psum", bufs=1))
+
+        def sbuf(name, shape, dtype, tag=None):
+            return keep.tile(shape, dtype, name=name, tag=tag or name, align_bytes=64)
+
+        def bank(name, tag):
+            return psum.tile([P, PACK, CHUNK], F32, name=name, tag=tag)
+
+        offsets = keep.tile([P, S // 16], U16, name="offsets")
+        nc.sync.dma_start(offsets[:], offs)
+
+        def load_gate(name, gate):
+            loaded = sbuf(name + "_loaded", [P, PACK], F32)
+            nc.sync.dma_start(loaded[:], gate.rearrange("(p t) o -> p (t o)", t=PACK))
+            spread = sbuf(name + "_cols", [P, CHUNK, PACK], F32)
+            nc.scalar.activation(spread[:], loaded[:].unsqueeze(1).to_broadcast([P, CHUNK, PACK]), COPY)
+            return loaded, spread
+
+        gt_loaded, gt_cols = load_gate("gt", gt)
+
+        word_table = sbuf("word_table", [P, T], I32)
+        word_rows = x_words[0].rearrange("p n t -> p (n t)").bitcast(I32)
+        nc.sync.dma_start(word_table[:, :LEAD], word_rows[:, :LEAD])
+
+        scale_table = sbuf("scale_table", [P, T], U8)
+        nc.vector.memset(scale_table[:, : T // 2].bitcast(I32), 0)
+        nc.gpsimd.memset(scale_table[:, T // 2 :].bitcast(I32), 0)
+        scale_rows = x_scales[0].bitcast(I32)
+        for q in range(4):
+            nc.sync.dma_start(scale_table[32 * q : 32 * q + 4, :].bitcast(I32), scale_rows[4 * q : 4 * q + 4, :])
+        nc.sync.dma_start(word_table[:, LEAD:], word_rows[:, LEAD:])
+
+        def load_weights(name, w, widths):
+            rows = w.rearrange("(p j) c -> p j c", j=PACK)
+            chunks, first = [], 0
+            for width in widths:
+                raw = sbuf(f"{name}_raw{first}", [P, PACK, width], F32)
+                nc.sync.dma_start(raw[:], rows[:, :, first : first + width])
+                chunks.extend(raw[:, :, c : c + CHUNK] for c in range(0, width, CHUNK))
+                first = first + width
+            return chunks
+
+        wa_raw = load_weights("wa", wa, (CHUNK, CHUNK, HALF))
+        gi_loaded = sbuf("gi_loaded", [P, PACK], F32)
+        nc.sync.dma_start(gi_loaded[:], gi.rearrange("(p t) o -> p (t o)", t=PACK))
+        gi_cols = gi_loaded[:].unsqueeze(1).to_broadcast([P, CHUNK, PACK])
+        wb_rows = wb.rearrange("(p j) c -> p j c", j=PACK)
+        wb_raw = []
+        for h in range(2):
+            wb_raw.append(sbuf(f"wb_raw{h}", [P, PACK, HALF], F32))
+            nc.sync.dma_start(wb_raw[h][:], wb_rows[:, :, h * HALF : (h + 1) * HALF])
+
+        picked_scales = sbuf("picked_scales", [P, S], U8)
+        nc.vector.tensor_copy(picked_scales[:], scale_table[:].indirect(offsets[:]))
+        x_scale = sbuf("x_scale", [P, S], U8)
+        nc.vector.tensor_copy(
+            x_scale[:].rearrange("p (t m) -> p t m", t=PACK),
+            picked_scales[:].rearrange("p (m t) -> p t m", t=PACK),
+        )
+        x_codes = sbuf("x_codes", [P, S], U32)
+        nc.vector.tensor_copy(
+            x_codes[:].rearrange("p (t m) -> p m t", t=PACK),
+            word_table[:].bitcast(U32).indirect(offsets[:]),
+        )
+
+        def quantize(name, rounded, width):
+            codes = sbuf(name + "_codes", [P, width], U32)
+            scales = sbuf(name + "_scales", [P, width], U8)
+            nc.vector.quantize_mx(out=codes[:].bitcast(FP8X4), scales=scales[:], in_=rounded)
+            return codes, scales
+
+        def product(acc, stationary, moving, cols):
+            for t in range(PACK):
+                part = slice(t * P, (t + 1) * P)
+                nc.tensor.matmul_mx(
+                    out=acc[:, t, :],
+                    lhsT=stationary[0][:, part].bitcast(FP8X4),
+                    lhsT_scale=stationary[1][:, part],
+                    rhs=moving[0][:, cols].bitcast(FP8X4),
+                    rhs_scale=moving[1][:, cols],
+                    start=True,
+                    stop=True,
+                )
+
+        x_mx = (x_codes, x_scale)
+
+        def chunk_cols(c):
+            return slice(c * CHUNK, (c + 1) * CHUNK)
+
+        wa_bf, wb_bf = [], []
+        for c in range(CHUNKS):
+            wa_bf.append(sbuf(f"wa_bf{c}", [P, CHUNK * PACK], BF16))
+            nc.scalar.copy(
+                wa_bf[c][:].rearrange("p (u m j) -> p m j u", u=PACK, j=PACK),
+                wa_raw[c].rearrange("p j (m u) -> p m j u", u=PACK),
+            )
+        for h in range(2):
+            wb_bf.append(sbuf(f"wb_bf{h}", [P, HALF * PACK], BF16))
+            nc.scalar.copy(
+                wb_bf[h][:].rearrange("p (c i j) -> p c j i", i=PACK, j=PACK),
+                wb_raw[h][:].rearrange("p j (c i) -> p c j i", i=PACK),
+            )
+
+        whole = slice(0, CHUNK)
+        a_banks = [bank(f"a{c}", f"lo{c}") for c in range(CHUNKS)]
+        b_banks = [bank(f"b{c}", f"hi{c}") for c in range(CHUNKS)]
+
+        def project_a(c):
+            product(a_banks[c], x_mx, quantize(f"wa{c}", wa_bf[c][:], CHUNK), whole)
+
+        def project_b(h):
+            wb_mx = quantize(f"wb{h}", wb_bf[h][:], HALF)
+            for i in range(2):
+                product(b_banks[2 * h + i], x_mx, wb_mx, chunk_cols(i))
+
+        z_bf = sbuf("z_bf", [P, H * PACK], BF16)
+        z_view = z_bf[:].rearrange("p (u c m t) -> p u c m t", u=PACK, c=CHUNKS, t=PACK)
+
+        def leave_a(c):
+            nc.vector.scalar_tensor_tensor(
+                out=z_view[:, :, c, :, :],
+                in0=a_banks[c][:].rearrange("p t (u m) -> p u m t", u=PACK),
+                scalar=0.0,
+                in1=gt_cols[:].rearrange("p (u m) t -> p u m t", u=PACK),
+                op0=ALU.max,
+                op1=ALU.mult,
+            )
+
+        z2_bf = []
+
+        def leave_b(c):
+            z2_bf.append(ring.tile([P, CHUNK * PACK], BF16, name=f"z2_bf{c}", tag="z2_bf", align_bytes=64))
+            nc.vector.tensor_tensor(
+                out=z2_bf[c][:].rearrange("p (n t) -> p n t", t=PACK),
+                in0=b_banks[c][:].rearrange("p t n -> p n t"),
+                in1=gi_cols,
+                op=ALU.mult,
+            )
+
+        y_codes = sbuf("y_codes", [P, H], U32)
+        y_scales = sbuf("y_scales", [P, H], U8)
+        out_rows = out_0.rearrange("(p t) n -> p t n", t=PACK)
+        y_bf = [sbuf(f"y_bf{c}", [P, CHUNK * PACK], BF16) for c in range(CHUNKS)]
+        y_f32 = [sbuf(f"y_f32_{c}", [P, PACK, CHUNK], F32) for c in range(CHUNKS)]
+
+        def pool(c, z_mx):
+            z2_mx = quantize(f"z2_{c}", z2_bf[c][:], CHUNK)
+            acc = bank(f"y{c}", f"lo{c}")
+            product(acc, z_mx, z2_mx, whole)
+            nc.scalar.activation(y_f32[c][:], acc[:], COPY, scale=OUT_SCALE)
+            nc.sync.dma_start(out_rows[:, :, chunk_cols(c)], y_f32[c][:])
+            if c < SCALAR_ROUNDS:
+                nc.scalar.activation(
+                    y_bf[c][:].rearrange("p (n t) -> p n t", t=PACK),
+                    acc[:].rearrange("p t n -> p n t"),
+                    COPY,
+                    scale=OUT_SCALE,
+                )
+
+        def round_y(c):
+            nc.vector.tensor_copy(
+                y_bf[c][:].rearrange("p (c i t) -> p c t i", i=PACK, t=PACK),
+                y_f32[c][:].rearrange("p t (c i) -> p c t i", i=PACK),
+            )
+
+        def quantize_y(c):
+            nc.vector.quantize_mx(
+                out=y_codes[:, chunk_cols(c)].bitcast(FP8X4), scales=y_scales[:, chunk_cols(c)], in_=y_bf[c][:]
+            )
+
+        project_a(0)
+        for c in range(CHUNKS):
+            if c + 1 < CHUNKS:
+                project_a(c + 1)
+            else:
+                project_b(0)
+            leave_a(c)
+        leave_b(0)
+        z_mx = quantize("z", z_bf[:], H)
+        project_b(1)
+        pool(0, z_mx)
+        for c in range(1, CHUNKS):
+            leave_b(c)
+            pool(c, z_mx)
+        for c in range(CHUNKS):
+            if c >= SCALAR_ROUNDS:
+                round_y(c)
+            if c > 0:
+                quantize_y(c - 1)
+        quantize_y(CHUNKS - 1)
+
+        code_rows = out_1[0].rearrange("p n t -> p (n t)").bitcast(I32)
+        last = H - CHUNK
+        nc.sync.dma_start(code_rows[:, :last], y_codes[:, :last].bitcast(I32))
+        nc.sync.dma_start(code_rows[:, last:], y_codes[:, last:].bitcast(I32))
+        scale_out = out_2[0].bitcast(I32)
+        for q in range(4):
+            queue = nc.scalar if q % 2 else nc.sync
+            queue.dma_start(scale_out[4 * q : 4 * q + 4, :], y_scales[32 * q : 32 * q + 4, :].bitcast(I32))

@@ -3,7 +3,7 @@ from contextlib import ExitStack
 import concourse.mybir as mybir
 
 K, T, S, H = 512, 2048, 512, 512
-FLOPS = 3 * 2 * 512 * 512 * 512
+FLOPS = 2 * K * S * H + 2 * K * S * H + 2 * S * H * H
 
 F32 = mybir.dt.float32
 BF16 = mybir.dt.bfloat16
@@ -17,11 +17,13 @@ COPY = mybir.ActivationFunctionType.Copy
 
 P = 128
 PACK = 4
-LEAD = 512
-SCALAR_ROUNDS = 1
-HALF = H // 2
+QUADRANT = 32
 CHUNK = 128
 CHUNKS = H // CHUNK
+HALF = H // 2
+SHARE = CHUNK // PACK
+LEAD = T // 4
+SCALAR_CHUNK = 0
 OUT_SCALE = 0.0625
 
 
@@ -31,58 +33,58 @@ def tile_picked_bilpool_relu_po_kernel(
     nc = tc.nc
     with ExitStack() as ctx:
         keep = ctx.enter_context(tc.tile_pool(name="keep", bufs=1))
-        ring = ctx.enter_context(tc.tile_pool(name="ring", bufs=2))
         psum = ctx.enter_context(tc.psum_pool(name="psum", bufs=1))
 
-        def sbuf(name, shape, dtype, tag=None):
-            return keep.tile(shape, dtype, name=name, tag=tag or name, align_bytes=64)
+        def sbuf(name, shape, dtype):
+            return keep.tile(shape, dtype, name=name, align_bytes=64)
 
         def bank(name, tag):
             return psum.tile([P, PACK, CHUNK], F32, name=name, tag=tag)
 
-        offsets = keep.tile([P, S // 16], U16, name="offsets")
-        nc.sync.dma_start(offsets[:], offs)
+        def chunk_cols(c, width=CHUNK):
+            return slice(c * width, (c + 1) * width)
 
         def load_gate(name, gate):
-            loaded = sbuf(name + "_loaded", [P, PACK], F32)
+            loaded = sbuf(name, [P, PACK], F32)
             nc.sync.dma_start(loaded[:], gate.rearrange("(p t) o -> p (t o)", t=PACK))
-            spread = sbuf(name + "_cols", [P, CHUNK, PACK], F32)
-            nc.scalar.activation(spread[:], loaded[:].unsqueeze(1).to_broadcast([P, CHUNK, PACK]), COPY)
-            return loaded, spread
+            return loaded
 
-        gt_loaded, gt_cols = load_gate("gt", gt)
+        def repeat_gate(name, loaded, columns):
+            repeated = sbuf(name, [P, columns, PACK], F32)
+            nc.scalar.activation(repeated[:], loaded[:].unsqueeze(1).to_broadcast([P, columns, PACK]), COPY)
+            return repeated
+
+        def load_weights(name, w):
+            rows = w.rearrange("(p j) c -> p j c", j=PACK)
+            chunks = []
+            for h in range(2):
+                raw = sbuf(f"{name}_raw{h}", [P, PACK, HALF], F32)
+                nc.sync.dma_start(raw[:], rows[:, :, chunk_cols(h, HALF)])
+                chunks.extend(raw[:, :, chunk_cols(i)] for i in range(HALF // CHUNK))
+            return chunks
+
+        offsets = keep.tile([P, S // 16], U16, name="offsets")
+        nc.sync.dma_start(offsets[:], offs)
+        gi_loaded = load_gate("gi_loaded", gi)
+        gi_cols = repeat_gate("gi_cols", gi_loaded, CHUNK)
 
         word_table = sbuf("word_table", [P, T], I32)
         word_rows = x_words[0].rearrange("p n t -> p (n t)").bitcast(I32)
         nc.sync.dma_start(word_table[:, :LEAD], word_rows[:, :LEAD])
 
         scale_table = sbuf("scale_table", [P, T], U8)
-        nc.vector.memset(scale_table[:, : T // 2].bitcast(I32), 0)
-        nc.gpsimd.memset(scale_table[:, T // 2 :].bitcast(I32), 0)
+        nc.vector.memset(scale_table[:].bitcast(I32), 0)
         scale_rows = x_scales[0].bitcast(I32)
-        for q in range(4):
-            nc.sync.dma_start(scale_table[32 * q : 32 * q + 4, :].bitcast(I32), scale_rows[4 * q : 4 * q + 4, :])
+        for q in range(P // QUADRANT):
+            nc.sync.dma_start(
+                scale_table[QUADRANT * q : QUADRANT * q + 4, :].bitcast(I32), scale_rows[4 * q : 4 * q + 4, :]
+            )
         nc.sync.dma_start(word_table[:, LEAD:], word_rows[:, LEAD:])
 
-        def load_weights(name, w, widths):
-            rows = w.rearrange("(p j) c -> p j c", j=PACK)
-            chunks, first = [], 0
-            for width in widths:
-                raw = sbuf(f"{name}_raw{first}", [P, PACK, width], F32)
-                nc.sync.dma_start(raw[:], rows[:, :, first : first + width])
-                chunks.extend(raw[:, :, c : c + CHUNK] for c in range(0, width, CHUNK))
-                first = first + width
-            return chunks
-
-        wa_raw = load_weights("wa", wa, (CHUNK, CHUNK, HALF))
-        gi_loaded = sbuf("gi_loaded", [P, PACK], F32)
-        nc.sync.dma_start(gi_loaded[:], gi.rearrange("(p t) o -> p (t o)", t=PACK))
-        gi_cols = gi_loaded[:].unsqueeze(1).to_broadcast([P, CHUNK, PACK])
-        wb_rows = wb.rearrange("(p j) c -> p j c", j=PACK)
-        wb_raw = []
-        for h in range(2):
-            wb_raw.append(sbuf(f"wb_raw{h}", [P, PACK, HALF], F32))
-            nc.sync.dma_start(wb_raw[h][:], wb_rows[:, :, h * HALF : (h + 1) * HALF])
+        wa_raw = load_weights("wa", wa)
+        gt_loaded = load_gate("gt_loaded", gt)
+        gt_cols = repeat_gate("gt_cols", gt_loaded, SHARE)
+        wb_raw = load_weights("wb", wb)
 
         picked_scales = sbuf("picked_scales", [P, S], U8)
         nc.vector.tensor_copy(picked_scales[:], scale_table[:].indirect(offsets[:]))
@@ -96,30 +98,7 @@ def tile_picked_bilpool_relu_po_kernel(
             x_codes[:].rearrange("p (t m) -> p m t", t=PACK),
             word_table[:].bitcast(U32).indirect(offsets[:]),
         )
-
-        def quantize(name, rounded, width):
-            codes = sbuf(name + "_codes", [P, width], U32)
-            scales = sbuf(name + "_scales", [P, width], U8)
-            nc.vector.quantize_mx(out=codes[:].bitcast(FP8X4), scales=scales[:], in_=rounded)
-            return codes, scales
-
-        def product(acc, stationary, moving, cols):
-            for t in range(PACK):
-                part = slice(t * P, (t + 1) * P)
-                nc.tensor.matmul_mx(
-                    out=acc[:, t, :],
-                    lhsT=stationary[0][:, part].bitcast(FP8X4),
-                    lhsT_scale=stationary[1][:, part],
-                    rhs=moving[0][:, cols].bitcast(FP8X4),
-                    rhs_scale=moving[1][:, cols],
-                    start=True,
-                    stop=True,
-                )
-
         x_mx = (x_codes, x_scale)
-
-        def chunk_cols(c):
-            return slice(c * CHUNK, (c + 1) * CHUNK)
 
         wa_bf, wb_bf = [], []
         for c in range(CHUNKS):
@@ -128,106 +107,112 @@ def tile_picked_bilpool_relu_po_kernel(
                 wa_bf[c][:].rearrange("p (u m j) -> p m j u", u=PACK, j=PACK),
                 wa_raw[c].rearrange("p j (m u) -> p m j u", u=PACK),
             )
-        for h in range(2):
-            wb_bf.append(sbuf(f"wb_bf{h}", [P, HALF * PACK], BF16))
+        for c in range(CHUNKS):
+            wb_bf.append(sbuf(f"wb_bf{c}", [P, CHUNK * PACK], BF16))
             nc.scalar.copy(
-                wb_bf[h][:].rearrange("p (c i j) -> p c j i", i=PACK, j=PACK),
-                wb_raw[h][:].rearrange("p j (c i) -> p c j i", i=PACK),
+                wb_bf[c][:].rearrange("p (g i j) -> p g j i", i=PACK, j=PACK),
+                wb_raw[c].rearrange("p j (g i) -> p g j i", i=PACK),
             )
 
-        whole = slice(0, CHUNK)
-        a_banks = [bank(f"a{c}", f"lo{c}") for c in range(CHUNKS)]
-        b_banks = [bank(f"b{c}", f"hi{c}") for c in range(CHUNKS)]
+        def quantize(name, rounded, width):
+            codes = sbuf(name + "_codes", [P, width], U32)
+            scales = sbuf(name + "_scales", [P, width], U8)
+            nc.vector.quantize_mx(out=codes[:].bitcast(FP8X4), scales=scales[:], in_=rounded[:])
+            return codes, scales
 
-        def project_a(c):
-            product(a_banks[c], x_mx, quantize(f"wa{c}", wa_bf[c][:], CHUNK), whole)
+        def product(acc, dealt, moving):
+            for t in range(PACK):
+                nc.tensor.matmul_mx(
+                    out=acc[:, t, :],
+                    lhsT=dealt[0][:, chunk_cols(t, P)].bitcast(FP8X4),
+                    lhsT_scale=dealt[1][:, chunk_cols(t, P)],
+                    rhs=moving[0][:].bitcast(FP8X4),
+                    rhs_scale=moving[1][:],
+                    start=True,
+                    stop=True,
+                )
 
-        def project_b(h):
-            wb_mx = quantize(f"wb{h}", wb_bf[h][:], HALF)
-            for i in range(2):
-                product(b_banks[2 * h + i], x_mx, wb_mx, chunk_cols(i))
+        a_banks = [bank(f"a{c}", f"first{c}") for c in range(CHUNKS)]
+        b_banks = [bank(f"b{c}", f"second{c}") for c in range(CHUNKS)]
+        for c in range(CHUNKS):
+            product(a_banks[c], x_mx, quantize(f"wa{c}", wa_bf[c], CHUNK))
+        for c in range(CHUNKS):
+            product(b_banks[c], x_mx, quantize(f"wb{c}", wb_bf[c], CHUNK))
 
         z_bf = sbuf("z_bf", [P, H * PACK], BF16)
         z_view = z_bf[:].rearrange("p (u c m t) -> p u c m t", u=PACK, c=CHUNKS, t=PACK)
-
-        def leave_a(c):
+        for c in range(CHUNKS):
             nc.vector.scalar_tensor_tensor(
                 out=z_view[:, :, c, :, :],
                 in0=a_banks[c][:].rearrange("p t (u m) -> p u m t", u=PACK),
                 scalar=0.0,
-                in1=gt_cols[:].rearrange("p (u m) t -> p u m t", u=PACK),
+                in1=gt_cols[:].unsqueeze(1).to_broadcast([P, PACK, SHARE, PACK]),
                 op0=ALU.max,
                 op1=ALU.mult,
             )
+        z_mx = quantize("z", z_bf, H)
 
-        z2_bf = []
+        z2_bf = [sbuf(f"z2_bf{c}", [P, CHUNK * PACK], BF16) for c in range(CHUNKS)]
 
-        def leave_b(c):
-            z2_bf.append(ring.tile([P, CHUNK * PACK], BF16, name=f"z2_bf{c}", tag="z2_bf", align_bytes=64))
-            nc.vector.tensor_tensor(
-                out=z2_bf[c][:].rearrange("p (n t) -> p n t", t=PACK),
-                in0=b_banks[c][:].rearrange("p t n -> p n t"),
-                in1=gi_cols,
-                op=ALU.mult,
-            )
+        def weigh_b(c):
+            if c == SCALAR_CHUNK:
+                for t in range(PACK):
+                    nc.scalar.activation(
+                        z2_bf[c][:, t::PACK], b_banks[c][:, t, :], COPY, scale=gi_loaded[:, t : t + 1]
+                    )
+            else:
+                nc.vector.tensor_tensor(
+                    out=z2_bf[c][:].rearrange("p (n t) -> p n t", t=PACK),
+                    in0=b_banks[c][:].rearrange("p t n -> p n t"),
+                    in1=gi_cols[:],
+                    op=ALU.mult,
+                )
 
-        y_codes = sbuf("y_codes", [P, H], U32)
-        y_scales = sbuf("y_scales", [P, H], U8)
         out_rows = out_0.rearrange("(p t) n -> p t n", t=PACK)
-        y_bf = [sbuf(f"y_bf{c}", [P, CHUNK * PACK], BF16) for c in range(CHUNKS)]
         y_f32 = [sbuf(f"y_f32_{c}", [P, PACK, CHUNK], F32) for c in range(CHUNKS)]
 
-        def pool(c, z_mx):
-            z2_mx = quantize(f"z2_{c}", z2_bf[c][:], CHUNK)
-            acc = bank(f"y{c}", f"lo{c}")
-            product(acc, z_mx, z2_mx, whole)
+        def pool_chunk(c):
+            acc = bank(f"y{c}", f"first{c}")
+            product(acc, z_mx, quantize(f"z2_{c}", z2_bf[c], CHUNK))
             nc.scalar.activation(y_f32[c][:], acc[:], COPY, scale=OUT_SCALE)
             nc.sync.dma_start(out_rows[:, :, chunk_cols(c)], y_f32[c][:])
-            if c < SCALAR_ROUNDS:
-                nc.scalar.activation(
-                    y_bf[c][:].rearrange("p (n t) -> p n t", t=PACK),
-                    acc[:].rearrange("p t n -> p n t"),
-                    COPY,
-                    scale=OUT_SCALE,
-                )
+
+        weigh_b(SCALAR_CHUNK)
+        for c in range(1, CHUNKS):
+            weigh_b(c)
+            pool_chunk(c)
+            if c == 2:
+                pool_chunk(SCALAR_CHUNK)
+
+        y_bf = sbuf("y_bf", [P, H * PACK], BF16)
+        y_codes = sbuf("y_codes", [P, H], U32)
+        y_scales = sbuf("y_scales", [P, H], U8)
+        code_rows = out_1[0].rearrange("p n t -> p (n t)").bitcast(I32)
 
         def round_y(c):
             nc.vector.tensor_copy(
-                y_bf[c][:].rearrange("p (c i t) -> p c t i", i=PACK, t=PACK),
-                y_f32[c][:].rearrange("p t (c i) -> p c t i", i=PACK),
+                y_bf[:, chunk_cols(c, CHUNK * PACK)].rearrange("p (g i t) -> p g t i", i=PACK, t=PACK),
+                y_f32[c][:].rearrange("p t (g i) -> p g t i", i=PACK),
             )
 
-        def quantize_y(c):
+        def quantize_y(first, last):
             nc.vector.quantize_mx(
-                out=y_codes[:, chunk_cols(c)].bitcast(FP8X4), scales=y_scales[:, chunk_cols(c)], in_=y_bf[c][:]
+                out=y_codes[:, first:last].bitcast(FP8X4),
+                scales=y_scales[:, first:last],
+                in_=y_bf[:, first * PACK : last * PACK],
             )
 
-        project_a(0)
-        for c in range(CHUNKS):
-            if c + 1 < CHUNKS:
-                project_a(c + 1)
-            else:
-                project_b(0)
-            leave_a(c)
-        leave_b(0)
-        z_mx = quantize("z", z_bf[:], H)
-        project_b(1)
-        pool(0, z_mx)
-        for c in range(1, CHUNKS):
-            leave_b(c)
-            pool(c, z_mx)
-        for c in range(CHUNKS):
-            if c >= SCALAR_ROUNDS:
-                round_y(c)
-            if c > 0:
-                quantize_y(c - 1)
-        quantize_y(CHUNKS - 1)
-
-        code_rows = out_1[0].rearrange("p n t -> p (n t)").bitcast(I32)
-        last = H - CHUNK
-        nc.sync.dma_start(code_rows[:, :last], y_codes[:, :last].bitcast(I32))
-        nc.sync.dma_start(code_rows[:, last:], y_codes[:, last:].bitcast(I32))
+        for c in (1, 0, 2):
+            round_y(c)
+        quantize_y(0, HALF)
+        nc.sync.dma_start(code_rows[:, :HALF], y_codes[:, :HALF].bitcast(I32))
+        round_y(CHUNKS - 1)
+        quantize_y(HALF, H - CHUNK)
+        quantize_y(H - CHUNK, H)
+        nc.sync.dma_start(code_rows[:, HALF:], y_codes[:, HALF:].bitcast(I32))
         scale_out = out_2[0].bitcast(I32)
-        for q in range(4):
+        for q in range(P // QUADRANT):
             queue = nc.scalar if q % 2 else nc.sync
-            queue.dma_start(scale_out[4 * q : 4 * q + 4, :], y_scales[32 * q : 32 * q + 4, :].bitcast(I32))
+            queue.dma_start(
+                scale_out[4 * q : 4 * q + 4, :], y_scales[QUADRANT * q : QUADRANT * q + 4, :].bitcast(I32)
+            )

@@ -65,12 +65,12 @@ def tile_picked_bilpool_relu_po_kernel(
 
         offsets = keep.tile([P, S // 16], U16, name="offsets")
         nc.sync.dma_start(offsets[:], offs)
-        gi_loaded = load_gate("gi_loaded", gi)
-        gi_cols = repeat_gate("gi_cols", gi_loaded, CHUNK)
-
         word_table = sbuf("word_table", [P, T], I32)
         word_rows = x_words[0].rearrange("p n t -> p (n t)").bitcast(I32)
         nc.sync.dma_start(word_table[:, :LEAD], word_rows[:, :LEAD])
+
+        gi_loaded = load_gate("gi_loaded", gi)
+        gi_cols = repeat_gate("gi_cols", gi_loaded, CHUNK)
 
         scale_table = sbuf("scale_table", [P, T], U8)
         nc.vector.memset(scale_table[:].bitcast(I32), 0)
@@ -205,11 +205,10 @@ def tile_picked_bilpool_relu_po_kernel(
         for c in (1, 0, 2):
             round_y(c)
         quantize_y(0, HALF)
-        nc.sync.dma_start(code_rows[:, :HALF], y_codes[:, :HALF].bitcast(I32))
         round_y(CHUNKS - 1)
         quantize_y(HALF, H - CHUNK)
         quantize_y(H - CHUNK, H)
-        nc.sync.dma_start(code_rows[:, HALF:], y_codes[:, HALF:].bitcast(I32))
+        nc.sync.dma_start(code_rows, y_codes[:].bitcast(I32))
         scale_out = out_2[0].bitcast(I32)
         for q in range(P // QUADRANT):
             queue = nc.scalar if q % 2 else nc.sync

@@ -35,8 +35,8 @@ def tile_picked_bilpool_relu_po_kernel(
         keep = ctx.enter_context(tc.tile_pool(name="keep", bufs=1))
         psum = ctx.enter_context(tc.psum_pool(name="psum", bufs=1))
 
-        def sbuf(name, shape, dtype):
-            return keep.tile(shape, dtype, name=name, align_bytes=64)
+        def sbuf(name, shape, dtype, tag=""):
+            return keep.tile(shape, dtype, name=name, tag=tag or name, align_bytes=64)
 
         def bank(name, tag):
             return psum.tile([P, PACK, CHUNK], F32, name=name, tag=tag)
@@ -49,19 +49,15 @@ def tile_picked_bilpool_relu_po_kernel(
             nc.sync.dma_start(loaded[:], gate.rearrange("(p t) o -> p (t o)", t=PACK))
             return loaded
 
-        def repeat_gate(name, loaded, columns):
-            repeated = sbuf(name, [P, columns, PACK], F32)
-            nc.scalar.activation(repeated[:], loaded[:].unsqueeze(1).to_broadcast([P, columns, PACK]), COPY)
-            return repeated
+        def repeat_gate(name, loaded, tag=""):
+            repeated = sbuf(name, [P, SHARE, PACK], F32, tag)
+            nc.scalar.activation(repeated[:], loaded[:].unsqueeze(1).to_broadcast([P, SHARE, PACK]), COPY)
+            return repeated[:].unsqueeze(1).to_broadcast([P, PACK, SHARE, PACK])
 
-        def load_weights(name, w):
-            rows = w.rearrange("(p j) c -> p j c", j=PACK)
-            chunks = []
-            for h in range(2):
-                raw = sbuf(f"{name}_raw{h}", [P, PACK, HALF], F32)
-                nc.sync.dma_start(raw[:], rows[:, :, chunk_cols(h, HALF)])
-                chunks.extend(raw[:, :, chunk_cols(i)] for i in range(HALF // CHUNK))
-            return chunks
+        def load_half(name, w, h):
+            raw = sbuf(f"{name}_raw{h}", [P, PACK, HALF], F32)
+            nc.sync.dma_start(raw[:], w.rearrange("(p j) c -> p j c", j=PACK)[:, :, chunk_cols(h, HALF)])
+            return [raw[:, :, chunk_cols(i)] for i in range(HALF // CHUNK)]
 
         offsets = keep.tile([P, S // 16], U16, name="offsets")
         nc.sync.dma_start(offsets[:], offs)
@@ -69,8 +65,8 @@ def tile_picked_bilpool_relu_po_kernel(
         word_rows = x_words[0].rearrange("p n t -> p (n t)").bitcast(I32)
         nc.sync.dma_start(word_table[:, :LEAD], word_rows[:, :LEAD])
 
-        gi_loaded = load_gate("gi_loaded", gi)
-        gi_cols = repeat_gate("gi_cols", gi_loaded, CHUNK)
+        gt_loaded = load_gate("gt_loaded", gt)
+        gt_first = repeat_gate("gt_first", gt_loaded)
 
         scale_table = sbuf("scale_table", [P, T], U8)
         nc.vector.memset(scale_table[:].bitcast(I32), 0)
@@ -81,10 +77,9 @@ def tile_picked_bilpool_relu_po_kernel(
             )
         nc.sync.dma_start(word_table[:, LEAD:], word_rows[:, LEAD:])
 
-        wa_raw = load_weights("wa", wa)
-        gt_loaded = load_gate("gt_loaded", gt)
-        gt_cols = repeat_gate("gt_cols", gt_loaded, SHARE)
-        wb_raw = load_weights("wb", wb)
+        wa_raw = load_half("wa", wa, 0) + load_half("wa", wa, 1)
+        wb_raw = load_half("wb", wb, 0) + load_half("wb", wb, 1)
+        gi_loaded = load_gate("gi_loaded", gi)
 
         picked_scales = sbuf("picked_scales", [P, S], U8)
         nc.vector.tensor_copy(picked_scales[:], scale_table[:].indirect(offsets[:]))
@@ -107,12 +102,17 @@ def tile_picked_bilpool_relu_po_kernel(
                 wa_bf[c][:].rearrange("p (u m j) -> p m j u", u=PACK, j=PACK),
                 wa_raw[c].rearrange("p j (m u) -> p m j u", u=PACK),
             )
+        gt_later = repeat_gate("gt_later", gt_loaded, tag="wa_raw1")
         for c in range(CHUNKS):
+            if c == 2:
+                gt_last = repeat_gate("gt_last", gt_loaded, tag="wb_raw0")
             wb_bf.append(sbuf(f"wb_bf{c}", [P, CHUNK * PACK], BF16))
             nc.scalar.copy(
                 wb_bf[c][:].rearrange("p (g i j) -> p g j i", i=PACK, j=PACK),
                 wb_raw[c].rearrange("p j (g i) -> p g j i", i=PACK),
             )
+
+        gi_cols = repeat_gate("gi_cols", gi_loaded)
 
         def quantize(name, rounded, width):
             codes = sbuf(name + "_codes", [P, width], U32)
@@ -146,7 +146,7 @@ def tile_picked_bilpool_relu_po_kernel(
                 out=z_view[:, :, c, :, :],
                 in0=a_banks[c][:].rearrange("p t (u m) -> p u m t", u=PACK),
                 scalar=0.0,
-                in1=gt_cols[:].unsqueeze(1).to_broadcast([P, PACK, SHARE, PACK]),
+                in1=(gt_first, gt_later, gt_later, gt_last)[c],
                 op0=ALU.max,
                 op1=ALU.mult,
             )
@@ -162,9 +162,9 @@ def tile_picked_bilpool_relu_po_kernel(
                     )
             else:
                 nc.vector.tensor_tensor(
-                    out=z2_bf[c][:].rearrange("p (n t) -> p n t", t=PACK),
-                    in0=b_banks[c][:].rearrange("p t n -> p n t"),
-                    in1=gi_cols[:],
+                    out=z2_bf[c][:].rearrange("p (u m t) -> p u m t", u=PACK, t=PACK),
+                    in0=b_banks[c][:].rearrange("p t (u m) -> p u m t", u=PACK),
+                    in1=gi_cols,
                     op=ALU.mult,
                 )
 

@@ -23,7 +23,7 @@ CHUNKS = H // CHUNK
 HALF = H // 2
 SHARE = CHUNK // PACK
 LEAD = T // 4
-SCALAR_CHUNK = 0
+SCALAR_CHUNK = 1
 OUT_SCALE = 0.0625
 
 
@@ -49,10 +49,14 @@ def tile_picked_bilpool_relu_po_kernel(
             nc.sync.dma_start(loaded[:], gate.rearrange("(p t) o -> p (t o)", t=PACK))
             return loaded
 
-        def repeat_gate(name, loaded, tag=""):
-            repeated = sbuf(name, [P, SHARE, PACK], F32, tag)
-            nc.scalar.activation(repeated[:], loaded[:].unsqueeze(1).to_broadcast([P, SHARE, PACK]), COPY)
-            return repeated[:].unsqueeze(1).to_broadcast([P, PACK, SHARE, PACK])
+        def repeat_gate(place, loaded):
+            nc.scalar.copy(
+                place.rearrange("p (m t) -> p m t", t=PACK), loaded[:].unsqueeze(1).to_broadcast([P, SHARE, PACK])
+            )
+            return place
+
+        def by_columns(table):
+            return table.rearrange("p (m t) -> p m t", t=PACK).unsqueeze(1).to_broadcast([P, PACK, SHARE, PACK])
 
         def load_half(name, w, h):
             raw = sbuf(f"{name}_raw{h}", [P, PACK, HALF], F32)
@@ -66,7 +70,7 @@ def tile_picked_bilpool_relu_po_kernel(
         nc.sync.dma_start(word_table[:, :LEAD], word_rows[:, :LEAD])
 
         gt_loaded = load_gate("gt_loaded", gt)
-        gt_first = repeat_gate("gt_first", gt_loaded)
+        gt_table = repeat_gate(sbuf("gt_table", [P, CHUNK], F32)[:], gt_loaded)
 
         scale_table = sbuf("scale_table", [P, T], U8)
         nc.vector.memset(scale_table[:].bitcast(I32), 0)
@@ -78,8 +82,9 @@ def tile_picked_bilpool_relu_po_kernel(
         nc.sync.dma_start(word_table[:, LEAD:], word_rows[:, LEAD:])
 
         wa_raw = load_half("wa", wa, 0) + load_half("wa", wa, 1)
-        wb_raw = load_half("wb", wb, 0) + load_half("wb", wb, 1)
+        wb_raw = load_half("wb", wb, 0)
         gi_loaded = load_gate("gi_loaded", gi)
+        wb_raw = wb_raw + load_half("wb", wb, 1)
 
         picked_scales = sbuf("picked_scales", [P, S], U8)
         nc.vector.tensor_copy(picked_scales[:], scale_table[:].indirect(offsets[:]))
@@ -95,27 +100,23 @@ def tile_picked_bilpool_relu_po_kernel(
         )
         x_mx = (x_codes, x_scale)
 
-        wa_bf, wb_bf = [], []
-        for c in range(CHUNKS):
-            wa_bf.append(sbuf(f"wa_bf{c}", [P, CHUNK * PACK], BF16))
-            nc.scalar.copy(
+        wa_bf = [sbuf(f"wa_bf{c}", [P, CHUNK * PACK], BF16) for c in range(CHUNKS)]
+        wb_bf = [sbuf(f"wb_bf{c}", [P, CHUNK * PACK], BF16) for c in range(CHUNKS)]
+
+        def round_wa(c, copy):
+            copy(
                 wa_bf[c][:].rearrange("p (u m j) -> p m j u", u=PACK, j=PACK),
                 wa_raw[c].rearrange("p j (m u) -> p m j u", u=PACK),
             )
-        gt_later = repeat_gate("gt_later", gt_loaded, tag="wa_raw1")
-        for c in range(CHUNKS):
-            if c == 2:
-                gt_last = repeat_gate("gt_last", gt_loaded, tag="wb_raw0")
-            wb_bf.append(sbuf(f"wb_bf{c}", [P, CHUNK * PACK], BF16))
-            nc.scalar.copy(
+
+        def round_wb(c, copy):
+            copy(
                 wb_bf[c][:].rearrange("p (g i j) -> p g j i", i=PACK, j=PACK),
                 wb_raw[c].rearrange("p j (g i) -> p g j i", i=PACK),
             )
 
-        gi_cols = repeat_gate("gi_cols", gi_loaded)
-
-        def quantize(name, rounded, width):
-            codes = sbuf(name + "_codes", [P, width], U32)
+        def quantize(name, rounded, width, tag=""):
+            codes = sbuf(name + "_codes", [P, width], U32, tag)
             scales = sbuf(name + "_scales", [P, width], U8)
             nc.vector.quantize_mx(out=codes[:].bitcast(FP8X4), scales=scales[:], in_=rounded[:])
             return codes, scales
@@ -134,55 +135,83 @@ def tile_picked_bilpool_relu_po_kernel(
 
         a_banks = [bank(f"a{c}", f"first{c}") for c in range(CHUNKS)]
         b_banks = [bank(f"b{c}", f"second{c}") for c in range(CHUNKS)]
-        for c in range(CHUNKS):
-            product(a_banks[c], x_mx, quantize(f"wa{c}", wa_bf[c], CHUNK))
-        for c in range(CHUNKS):
+
+        def project_a(c, tag=""):
+            product(a_banks[c], x_mx, quantize(f"wa{c}", wa_bf[c], CHUNK, tag))
+
+        def project_b(c):
             product(b_banks[c], x_mx, quantize(f"wb{c}", wb_bf[c], CHUNK))
 
         z_bf = sbuf("z_bf", [P, H * PACK], BF16)
         z_view = z_bf[:].rearrange("p (u c m t) -> p u c m t", u=PACK, c=CHUNKS, t=PACK)
-        for c in range(CHUNKS):
+
+        def weigh_a(c, table):
             nc.vector.scalar_tensor_tensor(
                 out=z_view[:, :, c, :, :],
                 in0=a_banks[c][:].rearrange("p t (u m) -> p u m t", u=PACK),
                 scalar=0.0,
-                in1=(gt_first, gt_later, gt_later, gt_last)[c],
+                in1=by_columns(table),
                 op0=ALU.max,
                 op1=ALU.mult,
             )
-        z_mx = quantize("z", z_bf, H)
 
-        z2_bf = [sbuf(f"z2_bf{c}", [P, CHUNK * PACK], BF16) for c in range(CHUNKS)]
+        z2_tags = ("z2_bf0", "z2_bf1", "wb_bf3", "z2_bf1")
+        z2_bf = [sbuf(f"z2_bf{c}", [P, CHUNK * PACK], BF16, z2_tags[c]) for c in range(CHUNKS)]
 
-        def weigh_b(c):
-            if c == SCALAR_CHUNK:
-                for t in range(PACK):
-                    nc.scalar.activation(
-                        z2_bf[c][:, t::PACK], b_banks[c][:, t, :], COPY, scale=gi_loaded[:, t : t + 1]
-                    )
-            else:
-                nc.vector.tensor_tensor(
-                    out=z2_bf[c][:].rearrange("p (u m t) -> p u m t", u=PACK, t=PACK),
-                    in0=b_banks[c][:].rearrange("p t (u m) -> p u m t", u=PACK),
-                    in1=gi_cols,
-                    op=ALU.mult,
-                )
+        def weigh_b(c, table):
+            nc.vector.tensor_tensor(
+                out=z2_bf[c][:].rearrange("p (u m t) -> p u m t", u=PACK, t=PACK),
+                in0=b_banks[c][:].rearrange("p t (u m) -> p u m t", u=PACK),
+                in1=by_columns(table),
+                op=ALU.mult,
+            )
+
+        def weigh_b_on_scalar(c, table):
+            for t in range(PACK):
+                nc.scalar.activation(z2_bf[c][:, t::PACK], b_banks[c][:, t, :], COPY, scale=table[:, t : t + 1])
 
         out_rows = out_0.rearrange("(p t) n -> p t n", t=PACK)
         y_f32 = [sbuf(f"y_f32_{c}", [P, PACK, CHUNK], F32) for c in range(CHUNKS)]
 
-        def pool_chunk(c):
+        def pool_chunk(c, z_mx):
             acc = bank(f"y{c}", f"first{c}")
             product(acc, z_mx, quantize(f"z2_{c}", z2_bf[c], CHUNK))
             nc.scalar.activation(y_f32[c][:], acc[:], COPY, scale=OUT_SCALE)
             nc.sync.dma_start(out_rows[:, :, chunk_cols(c)], y_f32[c][:])
 
-        weigh_b(SCALAR_CHUNK)
-        for c in range(1, CHUNKS):
-            weigh_b(c)
-            pool_chunk(c)
-            if c == 2:
-                pool_chunk(SCALAR_CHUNK)
+        round_wa(0, nc.scalar.copy)
+        round_wa(1, nc.vector.tensor_copy)
+        project_a(0)
+        project_a(1, tag="wa_raw0")
+        round_wa(2, nc.scalar.copy)
+        round_wa(3, nc.vector.tensor_copy)
+        gt_first = wa_raw[3][:, 0, :]
+        nc.vector.tensor_copy(gt_first, gt_table)
+        round_wb(0, nc.scalar.copy)
+        gt_last = repeat_gate(wb_raw[0][:, 0, :], gt_loaded)
+        round_wb(1, nc.scalar.copy)
+        round_wb(2, nc.scalar.copy)
+        gi_table = repeat_gate(wb_raw[2][:, 0, :], gi_loaded)
+        round_wb(3, nc.scalar.copy)
+        weigh_a(0, gt_first)
+        project_a(3)
+        project_a(2)
+        weigh_a(1, gt_first)
+        project_b(0)
+        weigh_a(3, gt_last)
+        project_b(1)
+        weigh_a(2, gt_last)
+        project_b(2)
+        weigh_b_on_scalar(1, gi_table)
+        weigh_b(0, gi_table)
+        z_mx = quantize("z", z_bf, H, tag="gi_loaded")
+        project_b(3)
+        pool_chunk(0, z_mx)
+        weigh_b(2, gi_table)
+        pool_chunk(1, z_mx)
+        pool_chunk(2, z_mx)
+        weigh_b(3, gi_table)
+        pool_chunk(3, z_mx)
 
         y_bf = sbuf("y_bf", [P, H * PACK], BF16)
         y_codes = sbuf("y_codes", [P, H], U32)
@@ -202,7 +231,7 @@ def tile_picked_bilpool_relu_po_kernel(
                 in_=y_bf[:, first * PACK : last * PACK],
             )
 
-        for c in (1, 0, 2):
+        for c in (0, 1, 2):
             round_y(c)
         quantize_y(0, HALF)
         round_y(CHUNKS - 1)

@@ -22,7 +22,7 @@ CHUNK = 128
 CHUNKS = H // CHUNK
 HALF = H // 2
 SHARE = CHUNK // PACK
-LEAD = T // 4
+LEAD = T // 2
 SCALAR_CHUNK = 1
 OUT_SCALE = 0.0625
 
@@ -86,12 +86,9 @@ def tile_picked_bilpool_relu_po_kernel(
         gi_loaded = load_gate("gi_loaded", gi)
         wb_raw = wb_raw + load_half("wb", wb, 1)
 
-        picked_scales = sbuf("picked_scales", [P, S], U8)
-        nc.vector.tensor_copy(picked_scales[:], scale_table[:].indirect(offsets[:]))
         x_scale = sbuf("x_scale", [P, S], U8)
         nc.vector.tensor_copy(
-            x_scale[:].rearrange("p (t m) -> p t m", t=PACK),
-            picked_scales[:].rearrange("p (m t) -> p t m", t=PACK),
+            x_scale[:].rearrange("p (t m) -> p m t", t=PACK), scale_table[:].indirect(offsets[:])
         )
         x_codes = sbuf("x_codes", [P, S], U32)
         nc.vector.tensor_copy(
@@ -179,28 +176,25 @@ def tile_picked_bilpool_relu_po_kernel(
             nc.scalar.activation(y_f32[c][:], acc[:], COPY, scale=OUT_SCALE)
             nc.sync.dma_start(out_rows[:, :, chunk_cols(c)], y_f32[c][:])
 
-        round_wa(0, nc.scalar.copy)
-        round_wa(1, nc.vector.tensor_copy)
-        project_a(0)
-        project_a(1, tag="wa_raw0")
-        round_wa(2, nc.scalar.copy)
-        round_wa(3, nc.vector.tensor_copy)
-        gt_first = wa_raw[3][:, 0, :]
-        nc.vector.tensor_copy(gt_first, gt_table)
+        for c in range(CHUNKS):
+            round_wa(c, nc.scalar.copy)
+        gt_second = repeat_gate(wa_raw[3][:, 0, :], gt_loaded)
         round_wb(0, nc.scalar.copy)
         gt_last = repeat_gate(wb_raw[0][:, 0, :], gt_loaded)
         round_wb(1, nc.scalar.copy)
         round_wb(2, nc.scalar.copy)
         gi_table = repeat_gate(wb_raw[2][:, 0, :], gi_loaded)
         round_wb(3, nc.scalar.copy)
-        weigh_a(0, gt_first)
-        project_a(3)
+        project_a(0)
+        project_a(1)
+        weigh_a(0, gt_table)
         project_a(2)
-        weigh_a(1, gt_first)
+        project_a(3)
+        weigh_a(1, gt_second)
         project_b(0)
-        weigh_a(3, gt_last)
-        project_b(1)
         weigh_a(2, gt_last)
+        project_b(1)
+        weigh_a(3, gt_last)
         project_b(2)
         weigh_b_on_scalar(1, gi_table)
         weigh_b(0, gi_table)

@@ -24,6 +24,7 @@ HALF = H // 2
 SHARE = CHUNK // PACK
 LEAD = T // 2
 SCALAR_CHUNK = 1
+RUN = 8
 OUT_SCALE = 0.0625
 
 
@@ -108,8 +109,8 @@ def tile_picked_bilpool_relu_po_kernel(
 
         def round_wb(c, copy):
             copy(
-                wb_bf[c][:].rearrange("p (g i j) -> p g j i", i=PACK, j=PACK),
-                wb_raw[c].rearrange("p j (g i) -> p g j i", i=PACK),
+                wb_bf[c][:].rearrange("p (g i j) -> p g j i", i=RUN, j=PACK),
+                wb_raw[c].rearrange("p j (g i) -> p g j i", i=RUN),
             )
 
         def quantize(name, rounded, width, tag=""):
@@ -214,8 +215,8 @@ def tile_picked_bilpool_relu_po_kernel(
 
         def round_y(c):
             nc.vector.tensor_copy(
-                y_bf[:, chunk_cols(c, CHUNK * PACK)].rearrange("p (g i t) -> p g t i", i=PACK, t=PACK),
-                y_f32[c][:].rearrange("p t (g i) -> p g t i", i=PACK),
+                y_bf[:, chunk_cols(c, CHUNK * PACK)].rearrange("p (g i t) -> p g t i", i=RUN, t=PACK),
+                y_f32[c][:].rearrange("p t (g i) -> p g t i", i=RUN),
             )
 
         def quantize_y(first, last):

@@ -18,14 +18,15 @@ COPY = mybir.ActivationFunctionType.Copy
 P = 128
 PACK = 4
 QUADRANT = 32
+BLOCK = 8
 CHUNK = 128
 CHUNKS = H // CHUNK
 HALF = H // 2
 SHARE = CHUNK // PACK
-LEAD = T // 2
-SCALAR_CHUNK = 1
 RUN = 8
 OUT_SCALE = 0.0625
+LEAD = T // 2
+PAIRED = (1, 2)
 
 
 def tile_picked_bilpool_relu_po_kernel(
@@ -39,10 +40,13 @@ def tile_picked_bilpool_relu_po_kernel(
         def sbuf(name, shape, dtype, tag=""):
             return keep.tile(shape, dtype, name=name, tag=tag or name, align_bytes=64)
 
+        def raw_half(name):
+            return sbuf(name, [P, PACK, HALF], F32)
+
         def bank(name, tag):
             return psum.tile([P, PACK, CHUNK], F32, name=name, tag=tag)
 
-        def chunk_cols(c, width=CHUNK):
+        def cols(c, width=CHUNK):
             return slice(c * width, (c + 1) * width)
 
         def load_gate(name, gate):
@@ -59,33 +63,56 @@ def tile_picked_bilpool_relu_po_kernel(
         def by_columns(table):
             return table.rearrange("p (m t) -> p m t", t=PACK).unsqueeze(1).to_broadcast([P, PACK, SHARE, PACK])
 
-        def load_half(name, w, h):
-            raw = sbuf(f"{name}_raw{h}", [P, PACK, HALF], F32)
-            nc.sync.dma_start(raw[:], w.rearrange("(p j) c -> p j c", j=PACK)[:, :, chunk_cols(h, HALF)])
-            return [raw[:, :, chunk_cols(i)] for i in range(HALF // CHUNK)]
+        def load_half(raw, w, h):
+            nc.sync.dma_start(raw[:], w.rearrange("(p j) c -> p j c", j=PACK)[:, :, cols(h, HALF)])
+            return [raw[:, :, cols(i)] for i in range(HALF // CHUNK)]
 
-        offsets = keep.tile([P, S // 16], U16, name="offsets")
-        nc.sync.dma_start(offsets[:], offs)
+        def round_rows(copy, rounded, rows):
+            copy(
+                rounded.rearrange("p (g i j) -> p g j i", i=RUN, j=PACK),
+                rows.rearrange("p j (g i) -> p g j i", i=RUN),
+            )
+
+        def quantize(name, rounded, width, tag=""):
+            codes = sbuf(name + "_codes", [P, width], U32, tag)
+            scales = sbuf(name + "_scales", [P, width], U8)
+            nc.vector.quantize_mx(out=codes[:].bitcast(FP8X4), scales=scales[:], in_=rounded)
+            return codes, scales
+
+        def slices(codes, scales, count):
+            return [(codes[:, cols(t, P)], scales[:, cols(t, P)]) for t in range(count)]
+
+        def product(acc, dealt, moving):
+            for t, (codes, scales) in enumerate(dealt):
+                nc.tensor.matmul_mx(
+                    out=acc[:, t, :],
+                    lhsT=codes.bitcast(FP8X4),
+                    lhsT_scale=scales,
+                    rhs=moving[0][:].bitcast(FP8X4),
+                    rhs_scale=moving[1][:],
+                    start=True,
+                    stop=True,
+                )
+
         word_table = sbuf("word_table", [P, T], I32)
         word_rows = x_words[0].rearrange("p n t -> p (n t)").bitcast(I32)
         nc.sync.dma_start(word_table[:, :LEAD], word_rows[:, :LEAD])
-
-        gt_loaded = load_gate("gt_loaded", gt)
-        gt_table = repeat_gate(sbuf("gt_table", [P, CHUNK], F32)[:], gt_loaded)
+        offsets = keep.tile([P, S // 16], U16, name="offsets")
+        nc.sync.dma_start(offsets[:], offs)
 
         scale_table = sbuf("scale_table", [P, T], U8)
         nc.vector.memset(scale_table[:].bitcast(I32), 0)
         scale_rows = x_scales[0].bitcast(I32)
-        for q in range(P // QUADRANT):
-            nc.sync.dma_start(
-                scale_table[QUADRANT * q : QUADRANT * q + 4, :].bitcast(I32), scale_rows[4 * q : 4 * q + 4, :]
-            )
-        nc.sync.dma_start(word_table[:, LEAD:], word_rows[:, LEAD:])
+        for r in range(PACK):
+            nc.sync.dma_start(scale_table[r:P:QUADRANT, :].bitcast(I32), scale_rows[r::PACK, :])
 
-        wa_raw = load_half("wa", wa, 0) + load_half("wa", wa, 1)
-        wb_raw = load_half("wb", wb, 0)
+        nc.sync.dma_start(word_table[:, LEAD:], word_rows[:, LEAD:])
+        wa_raw = load_half(raw_half("wa_raw0"), wa, 0)
+        gt_loaded = load_gate("gt_loaded", gt)
+        wa_raw = wa_raw + load_half(raw_half("wa_raw1"), wa, 1)
+        wb_raw = load_half(raw_half("wb_raw0"), wb, 0)
+        wb_raw = wb_raw + load_half(raw_half("wb_raw1"), wb, 1)
         gi_loaded = load_gate("gi_loaded", gi)
-        wb_raw = wb_raw + load_half("wb", wb, 1)
 
         x_scale = sbuf("x_scale", [P, S], U8)
         nc.vector.tensor_copy(
@@ -96,10 +123,15 @@ def tile_picked_bilpool_relu_po_kernel(
             x_codes[:].rearrange("p (t m) -> p m t", t=PACK),
             word_table[:].bitcast(U32).indirect(offsets[:]),
         )
-        x_mx = (x_codes, x_scale)
+        x_mx = slices(x_codes, x_scale, PACK)
+        z2_tags = ("z2_bf0", "z2_bf1", "z2_bf2", "pairs1")
+        wb_tags = ("wb_bf0", "wb_bf1", "wb_bf2", "wb_bf1")
+        wa_tags = ("wa_bf0", "wa_bf1", "wa_bf2", "wa_bf1")
 
-        wa_bf = [sbuf(f"wa_bf{c}", [P, CHUNK * PACK], BF16) for c in range(CHUNKS)]
-        wb_bf = [sbuf(f"wb_bf{c}", [P, CHUNK * PACK], BF16) for c in range(CHUNKS)]
+        wa_bf = [sbuf(f"wa_bf{c}", [P, CHUNK * PACK], BF16, wa_tags[c]) for c in range(CHUNKS)]
+        wb_bf = [sbuf(f"wb_bf{c}", [P, CHUNK * PACK], BF16, wb_tags[c]) for c in range(CHUNKS)]
+        a_banks = [bank(f"a{c}", f"first{c}") for c in range(CHUNKS)]
+        b_banks = [bank(f"b{c}", f"second{c}") for c in range(CHUNKS)]
 
         def round_wa(c, copy):
             copy(
@@ -108,37 +140,29 @@ def tile_picked_bilpool_relu_po_kernel(
             )
 
         def round_wb(c, copy):
-            copy(
-                wb_bf[c][:].rearrange("p (g i j) -> p g j i", i=RUN, j=PACK),
-                wb_raw[c].rearrange("p j (g i) -> p g j i", i=RUN),
+            round_rows(copy, wb_bf[c][:], wb_raw[c])
+
+        def sbuf_copy(place, table):
+            nc.scalar.copy(place, table)
+            return place
+
+        def gpsimd_round(rounded, rows):
+            nc.gpsimd.tensor_scalar(rounded, rows, 1.0, 0.0, ALU.mult, ALU.add)
+
+        def round_wb_on_gpsimd(c):
+            gpsimd_round(wb_bf[c][:].rearrange("p (n j) -> p n j", j=PACK), wb_raw[c].rearrange("p j n -> p n j"))
+
+        def round_wa_on_gpsimd(c):
+            gpsimd_round(
+                wa_bf[c][:].rearrange("p (u m j) -> p u m j", u=PACK, j=PACK),
+                wa_raw[c].rearrange("p j (m u) -> p u m j", u=PACK),
             )
 
-        def quantize(name, rounded, width, tag=""):
-            codes = sbuf(name + "_codes", [P, width], U32, tag)
-            scales = sbuf(name + "_scales", [P, width], U8)
-            nc.vector.quantize_mx(out=codes[:].bitcast(FP8X4), scales=scales[:], in_=rounded[:])
-            return codes, scales
-
-        def product(acc, dealt, moving):
-            for t in range(PACK):
-                nc.tensor.matmul_mx(
-                    out=acc[:, t, :],
-                    lhsT=dealt[0][:, chunk_cols(t, P)].bitcast(FP8X4),
-                    lhsT_scale=dealt[1][:, chunk_cols(t, P)],
-                    rhs=moving[0][:].bitcast(FP8X4),
-                    rhs_scale=moving[1][:],
-                    start=True,
-                    stop=True,
-                )
-
-        a_banks = [bank(f"a{c}", f"first{c}") for c in range(CHUNKS)]
-        b_banks = [bank(f"b{c}", f"second{c}") for c in range(CHUNKS)]
-
         def project_a(c, tag=""):
-            product(a_banks[c], x_mx, quantize(f"wa{c}", wa_bf[c], CHUNK, tag))
+            product(a_banks[c], x_mx, quantize(f"wa{c}", wa_bf[c][:], CHUNK, tag))
 
-        def project_b(c):
-            product(b_banks[c], x_mx, quantize(f"wb{c}", wb_bf[c], CHUNK))
+        def project_b(c, tag=""):
+            product(b_banks[c], x_mx, quantize(f"wb{c}", wb_bf[c][:], CHUNK, tag))
 
         z_bf = sbuf("z_bf", [P, H * PACK], BF16)
         z_view = z_bf[:].rearrange("p (u c m t) -> p u c m t", u=PACK, c=CHUNKS, t=PACK)
@@ -153,7 +177,10 @@ def tile_picked_bilpool_relu_po_kernel(
                 op1=ALU.mult,
             )
 
-        z2_tags = ("z2_bf0", "z2_bf1", "wb_bf3", "z2_bf1")
+        pair_planes = {c: sbuf(f"pairs{c}", [P, 2, CHUNK, 2], BF16) for c in PAIRED}
+        def quantize_z(h, tag):
+            return slices(*quantize(f"z{h}", z_bf[:, cols(h, HALF * PACK)], HALF, tag), PACK // 2)
+
         z2_bf = [sbuf(f"z2_bf{c}", [P, CHUNK * PACK], BF16, z2_tags[c]) for c in range(CHUNKS)]
 
         def weigh_b(c, table):
@@ -168,45 +195,72 @@ def tile_picked_bilpool_relu_po_kernel(
             for t in range(PACK):
                 nc.scalar.activation(z2_bf[c][:, t::PACK], b_banks[c][:, t, :], COPY, scale=table[:, t : t + 1])
 
+        def weigh_b_in_pairs(c, table):
+            pairs = pair_planes[c]
+            for t in (0, 2, 1, 3):
+                nc.scalar.activation(
+                    pairs[:, t // 2, :, t % 2], b_banks[c][:, t, :], COPY, scale=table[:, t : t + 1]
+                )
+            return pairs
+
+        def weave(c, pairs):
+            nc.vector.tensor_copy(
+                z2_bf[c][:].bitcast(I32).rearrange("p (n u) -> p n u", u=2),
+                pairs[:].rearrange("p u n e -> p (u n e)").bitcast(I32).rearrange("p (u n) -> p n u", u=2),
+            )
+
         out_rows = out_0.rearrange("(p t) n -> p t n", t=PACK)
         y_f32 = [sbuf(f"y_f32_{c}", [P, PACK, CHUNK], F32) for c in range(CHUNKS)]
 
-        def pool_chunk(c, z_mx):
-            acc = bank(f"y{c}", f"first{c}")
-            product(acc, z_mx, quantize(f"z2_{c}", z2_bf[c], CHUNK))
-            nc.scalar.activation(y_f32[c][:], acc[:], COPY, scale=OUT_SCALE)
-            nc.sync.dma_start(out_rows[:, :, chunk_cols(c)], y_f32[c][:])
+        def quantize_z2(c):
+            return quantize(f"z2_{c}", z2_bf[c][:], CHUNK)
 
-        for c in range(CHUNKS):
-            round_wa(c, nc.scalar.copy)
-        gt_second = repeat_gate(wa_raw[3][:, 0, :], gt_loaded)
-        round_wb(0, nc.scalar.copy)
-        gt_last = repeat_gate(wb_raw[0][:, 0, :], gt_loaded)
-        round_wb(1, nc.scalar.copy)
-        round_wb(2, nc.scalar.copy)
-        gi_table = repeat_gate(wb_raw[2][:, 0, :], gi_loaded)
-        round_wb(3, nc.scalar.copy)
+        def pool_chunk(c, z_mx, moving):
+            acc = bank(f"y{c}", f"first{c}")
+            product(acc, z_mx, moving)
+            nc.scalar.activation(y_f32[c][:], acc[:], COPY, scale=OUT_SCALE)
+            nc.sync.dma_start(out_rows[:, :, cols(c)], y_f32[c][:])
+
+        round_wa(0, nc.scalar.copy)
+        round_wa(1, nc.scalar.copy)
+        gt_table = repeat_gate(sbuf("gt_table", [P, CHUNK], F32)[:], gt_loaded)
+        round_wa(2, nc.scalar.copy)
         project_a(0)
         project_a(1)
+        round_wa_on_gpsimd(3)
+        gt_second = wa_raw[3][:, 0, :]
+        gpsimd_round(gt_second, gt_table)
+        round_wb(0, nc.scalar.copy)
+        round_wb(1, nc.scalar.copy)
+        gt_late = sbuf_copy(wb_raw[0][:, 1, :], gt_table)
+        round_wb(2, nc.scalar.copy)
         weigh_a(0, gt_table)
         project_a(2)
         project_a(3)
         weigh_a(1, gt_second)
         project_b(0)
-        weigh_a(2, gt_last)
         project_b(1)
-        weigh_a(3, gt_last)
+        round_wb_on_gpsimd(3)
+        weigh_a(2, gt_late)
+        weigh_a(3, gt_late)
         project_b(2)
-        weigh_b_on_scalar(1, gi_table)
-        weigh_b(0, gi_table)
-        z_mx = quantize("z", z_bf, H, tag="gi_loaded")
         project_b(3)
-        pool_chunk(0, z_mx)
-        weigh_b(2, gi_table)
-        pool_chunk(1, z_mx)
-        pool_chunk(2, z_mx)
+        gi_table = repeat_gate(sbuf("gi_table", [P, CHUNK], F32)[:], gi_loaded)
+        weigh_b(0, gi_table)
+        pairs = {c: weigh_b_in_pairs(c, gi_table) for c in PAIRED}
+        z_mx = quantize_z(0, "wb_raw1")
+        first = quantize_z2(0)
+        weave(1, pairs[1])
+        z_mx = z_mx + quantize_z(1, "gi_loaded")
+        pool_chunk(0, z_mx, first)
+        pool_chunk(1, z_mx, quantize_z2(1))
         weigh_b(3, gi_table)
-        pool_chunk(3, z_mx)
+        weave(2, pairs[2])
+        pool_chunk(3, z_mx, quantize_z2(3))
+        last = quantize_z2(2)
+        y_again = bank("y_again", "second0")
+        product(y_again, z_mx, last)
+        pool_chunk(2, z_mx, last)
 
         y_bf = sbuf("y_bf", [P, H * PACK], BF16)
         y_codes = sbuf("y_codes", [P, H], U32)
@@ -214,10 +268,7 @@ def tile_picked_bilpool_relu_po_kernel(
         code_rows = out_1[0].rearrange("p n t -> p (n t)").bitcast(I32)
 
         def round_y(c):
-            nc.vector.tensor_copy(
-                y_bf[:, chunk_cols(c, CHUNK * PACK)].rearrange("p (g i t) -> p g t i", i=RUN, t=PACK),
-                y_f32[c][:].rearrange("p t (g i) -> p g t i", i=RUN),
-            )
+            round_rows(nc.vector.tensor_copy, y_bf[:, cols(c, CHUNK * PACK)], y_f32[c][:])
 
         def quantize_y(first, last):
             nc.vector.quantize_mx(
@@ -226,10 +277,17 @@ def tile_picked_bilpool_relu_po_kernel(
                 in_=y_bf[:, first * PACK : last * PACK],
             )
 
-        for c in (0, 1, 2):
-            round_y(c)
+        round_y(0)
+        round_y(1)
+        nc.vector.tensor_scalar(
+            y_bf[:, cols(2, CHUNK * PACK)].rearrange("p (n t) -> p n t", t=PACK),
+            y_again[:].rearrange("p t n -> p n t"),
+            OUT_SCALE,
+            None,
+            ALU.mult,
+        )
         quantize_y(0, HALF)
-        round_y(CHUNKS - 1)
+        round_y(3)
         quantize_y(HALF, H - CHUNK)
         quantize_y(H - CHUNK, H)
         nc.sync.dma_start(code_rows, y_codes[:].bitcast(I32))

@@ -154,8 +154,8 @@ def tile_picked_bilpool_relu_po_kernel(
 
         def round_wa_on_gpsimd(c):
             gpsimd_round(
-                wa_bf[c][:].rearrange("p (u m j) -> p u m j", u=PACK, j=PACK),
-                wa_raw[c].rearrange("p j (m u) -> p u m j", u=PACK),
+                wa_bf[c][:].rearrange("p (u m j) -> p m u j", u=PACK, j=PACK),
+                wa_raw[c].rearrange("p j (m u) -> p m u j", u=PACK),
             )
 
         def project_a(c, tag=""):

@@ -25,8 +25,9 @@ HALF = H // 2
 SHARE = CHUNK // PACK
 RUN = 8
 OUT_SCALE = 0.0625
-LEAD = T // 2
+LEAD = T // 4
 PAIRED = (1, 2)
+RAW_BYTES = PACK * HALF * 4
 
 
 def tile_picked_bilpool_relu_po_kernel(
@@ -35,6 +36,7 @@ def tile_picked_bilpool_relu_po_kernel(
     nc = tc.nc
     with ExitStack() as ctx:
         keep = ctx.enter_context(tc.tile_pool(name="keep", bufs=1))
+        placed = ctx.enter_context(tc.tile_pool(name="placed", bufs=1))
         psum = ctx.enter_context(tc.psum_pool(name="psum", bufs=1))
 
         def sbuf(name, shape, dtype, tag=""):
@@ -43,14 +45,17 @@ def tile_picked_bilpool_relu_po_kernel(
         def raw_half(name):
             return sbuf(name, [P, PACK, HALF], F32)
 
+        def at(offset, name, shape, dtype):
+            return placed.tile(shape, dtype, name=name, offset=offset, align_bytes=64)
+
         def bank(name, tag):
             return psum.tile([P, PACK, CHUNK], F32, name=name, tag=tag)
 
         def cols(c, width=CHUNK):
             return slice(c * width, (c + 1) * width)
 
-        def load_gate(name, gate):
-            loaded = sbuf(name, [P, PACK], F32)
+        def load_gate(name, gate, tag=""):
+            loaded = sbuf(name, [P, PACK], F32, tag)
             nc.sync.dma_start(loaded[:], gate.rearrange("(p t) o -> p (t o)", t=PACK))
             return loaded
 
@@ -74,7 +79,10 @@ def tile_picked_bilpool_relu_po_kernel(
             )
 
         def quantize(name, rounded, width, tag=""):
-            codes = sbuf(name + "_codes", [P, width], U32, tag)
+            if isinstance(tag, int):
+                codes = at(tag, name + "_codes", [P, width], U32)
+            else:
+                codes = sbuf(name + "_codes", [P, width], U32, tag)
             scales = sbuf(name + "_scales", [P, width], U8)
             nc.vector.quantize_mx(out=codes[:].bitcast(FP8X4), scales=scales[:], in_=rounded)
             return codes, scales
@@ -100,24 +108,29 @@ def tile_picked_bilpool_relu_po_kernel(
         offsets = keep.tile([P, S // 16], U16, name="offsets")
         nc.sync.dma_start(offsets[:], offs)
 
-        scale_table = sbuf("scale_table", [P, T], U8)
+        scale_table = at(RAW_BYTES - T // 2, "scale_table", [P, T], U8)
         nc.vector.memset(scale_table[:].bitcast(I32), 0)
-        scale_rows = x_scales[0].bitcast(I32)
-        for r in range(PACK):
-            nc.sync.dma_start(scale_table[r:P:QUADRANT, :].bitcast(I32), scale_rows[r::PACK, :])
+        x_scale = sbuf("x_scale", [P, S], U8)
+        nc.vector.memset(x_scale[:].bitcast(I32), 0)
+        nc.sync.dma_start(scale_table[0:P:BLOCK, :].bitcast(I32), x_scales[0].bitcast(I32))
 
         nc.sync.dma_start(word_table[:, LEAD:], word_rows[:, LEAD:])
         wa_raw = load_half(raw_half("wa_raw0"), wa, 0)
         gt_loaded = load_gate("gt_loaded", gt)
         wa_raw = wa_raw + load_half(raw_half("wa_raw1"), wa, 1)
-        wb_raw = load_half(raw_half("wb_raw0"), wb, 0)
-        wb_raw = wb_raw + load_half(raw_half("wb_raw1"), wb, 1)
-        gi_loaded = load_gate("gi_loaded", gi)
 
-        x_scale = sbuf("x_scale", [P, S], U8)
+        picked_scale = sbuf("picked_scale", [P, S], U8)
         nc.vector.tensor_copy(
-            x_scale[:].rearrange("p (t m) -> p m t", t=PACK), scale_table[:].indirect(offsets[:])
+            picked_scale[:].rearrange("p (t m) -> p m t", t=PACK), scale_table[:].indirect(offsets[:])
         )
+        for r in range(PACK):
+            nc.sync.dma_start(
+                x_scale[r:P:QUADRANT, :].bitcast(I32), picked_scale[BLOCK * r : P : QUADRANT, :].bitcast(I32)
+            )
+        wb_raw = load_half(at(0, "wb_raw0", [P, PACK, HALF], F32), wb, 0)
+        wb_raw = wb_raw + load_half(at(RAW_BYTES, "wb_raw1", [P, PACK, HALF], F32), wb, 1)
+        gi_loaded = load_gate("gi_loaded", gi, "picked_scale")
+
         x_codes = sbuf("x_codes", [P, S], U32)
         nc.vector.tensor_copy(
             x_codes[:].rearrange("p (t m) -> p m t", t=PACK),
@@ -225,11 +238,10 @@ def tile_picked_bilpool_relu_po_kernel(
         round_wa(1, nc.scalar.copy)
         gt_table = repeat_gate(sbuf("gt_table", [P, CHUNK], F32)[:], gt_loaded)
         round_wa(2, nc.scalar.copy)
+        gt_second = sbuf_copy(wa_raw[2][:, 0, :], gt_table)
         project_a(0)
         project_a(1)
         round_wa_on_gpsimd(3)
-        gt_second = wa_raw[3][:, 0, :]
-        gpsimd_round(gt_second, gt_table)
         round_wb(0, nc.scalar.copy)
         round_wb(1, nc.scalar.copy)
         gt_late = sbuf_copy(wb_raw[0][:, 1, :], gt_table)
@@ -248,10 +260,10 @@ def tile_picked_bilpool_relu_po_kernel(
         gi_table = repeat_gate(sbuf("gi_table", [P, CHUNK], F32)[:], gi_loaded)
         weigh_b(0, gi_table)
         pairs = {c: weigh_b_in_pairs(c, gi_table) for c in PAIRED}
-        z_mx = quantize_z(0, "wb_raw1")
+        z_mx = quantize_z(0, RAW_BYTES)
         first = quantize_z2(0)
         weave(1, pairs[1])
-        z_mx = z_mx + quantize_z(1, "gi_loaded")
+        z_mx = z_mx + quantize_z(1, "picked_scale")
         pool_chunk(0, z_mx, first)
         pool_chunk(1, z_mx, quantize_z2(1))
         weigh_b(3, gi_table)

@@ -139,7 +139,7 @@ def tile_picked_bilpool_relu_po_kernel(
         x_mx = slices(x_codes, x_scale, PACK)
         z2_tags = ("z2_bf0", "z2_bf1", "z2_bf2", "pairs1")
         wb_tags = ("wb_bf0", "wb_bf1", "wb_bf2", "wb_bf1")
-        wa_tags = ("wa_bf0", "wa_bf1", "wa_bf2", "wa_bf1")
+        wa_tags = ("wa_bf0", "wa_bf1", "wa_bf2", "wa_bf0")
 
         wa_bf = [sbuf(f"wa_bf{c}", [P, CHUNK * PACK], BF16, wa_tags[c]) for c in range(CHUNKS)]
         wb_bf = [sbuf(f"wb_bf{c}", [P, CHUNK * PACK], BF16, wb_tags[c]) for c in range(CHUNKS)]
@@ -154,10 +154,6 @@ def tile_picked_bilpool_relu_po_kernel(
 
         def round_wb(c, copy):
             round_rows(copy, wb_bf[c][:], wb_raw[c])
-
-        def sbuf_copy(place, table):
-            nc.scalar.copy(place, table)
-            return place
 
         def gpsimd_round(rounded, rows):
             nc.gpsimd.tensor_scalar(rounded, rows, 1.0, 0.0, ALU.mult, ALU.add)
@@ -236,20 +232,19 @@ def tile_picked_bilpool_relu_po_kernel(
 
         round_wa(0, nc.scalar.copy)
         round_wa(1, nc.scalar.copy)
-        gt_table = repeat_gate(sbuf("gt_table", [P, CHUNK], F32)[:], gt_loaded)
         round_wa(2, nc.scalar.copy)
-        gt_second = sbuf_copy(wa_raw[2][:, 0, :], gt_table)
+        gt_early = repeat_gate(wa_raw[2][:, 0, :], gt_loaded)
         project_a(0)
         project_a(1)
         round_wa_on_gpsimd(3)
         round_wb(0, nc.scalar.copy)
         round_wb(1, nc.scalar.copy)
-        gt_late = sbuf_copy(wb_raw[0][:, 1, :], gt_table)
+        gt_late = repeat_gate(wb_raw[0][:, 0, :], gt_loaded)
         round_wb(2, nc.scalar.copy)
-        weigh_a(0, gt_table)
         project_a(2)
         project_a(3)
-        weigh_a(1, gt_second)
+        weigh_a(0, gt_early)
+        weigh_a(1, gt_early)
         project_b(0)
         project_b(1)
         round_wb_on_gpsimd(3)
@@ -298,10 +293,9 @@ def tile_picked_bilpool_relu_po_kernel(
             None,
             ALU.mult,
         )
-        quantize_y(0, HALF)
         round_y(3)
-        quantize_y(HALF, H - CHUNK)
-        quantize_y(H - CHUNK, H)
+        quantize_y(0, HALF)
+        quantize_y(HALF, H)
         nc.sync.dma_start(code_rows, y_codes[:].bitcast(I32))
         scale_out = out_2[0].bitcast(I32)
         for q in range(P // QUADRANT):

@@ -224,6 +224,14 @@ def tile_picked_bilpool_relu_po_kernel(
         def quantize_z2(c):
             return quantize(f"z2_{c}", z2_bf[c][:], CHUNK)
 
+        def pool_first_chunk(z_mx, moving):
+            for h, tag in enumerate(("first0", "second1")):
+                rows = cols(h, PACK // 2)
+                acc = psum.tile([P, PACK // 2, CHUNK], F32, name=f"y0_{h}", tag=tag)
+                product(acc, z_mx[rows], moving)
+                nc.scalar.activation(y_f32[0][:, rows, :], acc[:], COPY, scale=OUT_SCALE)
+            nc.sync.dma_start(out_rows[:, :, cols(0)], y_f32[0][:])
+
         def pool_chunk(c, z_mx, moving):
             acc = bank(f"y{c}", f"first{c}")
             product(acc, z_mx, moving)
@@ -259,7 +267,7 @@ def tile_picked_bilpool_relu_po_kernel(
         first = quantize_z2(0)
         weave(1, pairs[1])
         z_mx = z_mx + quantize_z(1, "picked_scale")
-        pool_chunk(0, z_mx, first)
+        pool_first_chunk(z_mx, first)
         pool_chunk(1, z_mx, quantize_z2(1))
         weigh_b(3, gi_table)
         weave(2, pairs[2])
@@ -269,7 +277,7 @@ def tile_picked_bilpool_relu_po_kernel(
         product(y_again, z_mx, last)
         pool_chunk(2, z_mx, last)
 
-        y_bf = sbuf("y_bf", [P, H * PACK], BF16)
+        y_bf = sbuf("y_bf", [P, H * PACK], BF16, "pairs1")
         y_codes = sbuf("y_codes", [P, H], U32)
         y_scales = sbuf("y_scales", [P, H], U8)
         code_rows = out_1[0].rearrange("p n t -> p (n t)").bitcast(I32)

@@ -246,8 +246,8 @@ def tile_picked_bilpool_relu_po_kernel(
         project_a(1)
         round_wa_on_gpsimd(3)
         round_wb(0, nc.scalar.copy)
-        round_wb(1, nc.scalar.copy)
-        gt_late = repeat_gate(wb_raw[0][:, 0, :], gt_loaded)
+        round_wb_on_gpsimd(1)
+        gt_late = repeat_gate(at(0, "gt_late", [P, CHUNK], F32)[:], gt_loaded)
         round_wb(2, nc.scalar.copy)
         project_a(2)
         project_a(3)

@@ -116,8 +116,8 @@ def tile_picked_bilpool_relu_po_kernel(
 
         nc.sync.dma_start(word_table[:, LEAD:], word_rows[:, LEAD:])
         wa_raw = load_half(raw_half("wa_raw0"), wa, 0)
-        gt_loaded = load_gate("gt_loaded", gt)
         wa_raw = wa_raw + load_half(raw_half("wa_raw1"), wa, 1)
+        gt_loaded = load_gate("gt_loaded", gt)
 
         picked_scale = sbuf("picked_scale", [P, S], U8)
         nc.vector.tensor_copy(
@@ -138,11 +138,12 @@ def tile_picked_bilpool_relu_po_kernel(
         )
         x_mx = slices(x_codes, x_scale, PACK)
         z2_tags = ("z2_bf0", "z2_bf1", "z2_bf2", "pairs1")
-        wb_tags = ("wb_bf0", "wb_bf1", "wb_bf2", "wb_bf1")
         wa_tags = ("wa_bf0", "wa_bf1", "wa_bf2", "wa_bf0")
 
         wa_bf = [sbuf(f"wa_bf{c}", [P, CHUNK * PACK], BF16, wa_tags[c]) for c in range(CHUNKS)]
-        wb_bf = [sbuf(f"wb_bf{c}", [P, CHUNK * PACK], BF16, wb_tags[c]) for c in range(CHUNKS)]
+        wb_early = sbuf("wb_early", [P, HALF * PACK], BF16)
+        wb_bf = [wb_early[:, cols(c, CHUNK * PACK)] for c in range(2)]
+        wb_bf = wb_bf + [sbuf("wb_bf2", [P, CHUNK * PACK], BF16), sbuf("wb_bf3", [P, CHUNK * PACK], BF16, "wb_early")]
         a_banks = [bank(f"a{c}", f"first{c}") for c in range(CHUNKS)]
         b_banks = [bank(f"b{c}", f"second{c}") for c in range(CHUNKS)]
 
@@ -219,7 +220,9 @@ def tile_picked_bilpool_relu_po_kernel(
             )
 
         out_rows = out_0.rearrange("(p t) n -> p t n", t=PACK)
-        y_f32 = [sbuf(f"y_f32_{c}", [P, PACK, CHUNK], F32) for c in range(CHUNKS)]
+        y_early = sbuf("y_early", [P, PACK, HALF], F32)
+        y_f32 = [y_early[:, :, cols(c)] for c in range(2)]
+        y_f32 = y_f32 + [sbuf(f"y_f32_{c}", [P, PACK, CHUNK], F32) for c in range(2, CHUNKS)]
 
         def quantize_z2(c):
             return quantize(f"z2_{c}", z2_bf[c][:], CHUNK)
@@ -253,20 +256,24 @@ def tile_picked_bilpool_relu_po_kernel(
         project_a(3)
         weigh_a(0, gt_early)
         weigh_a(1, gt_early)
-        project_b(0)
-        project_b(1)
+        early = slices(*quantize("wb01", wb_early[:], HALF), 2)
+        product(b_banks[1], x_mx, early[1])
+        product(b_banks[0], x_mx, early[0])
         round_wb_on_gpsimd(3)
         weigh_a(2, gt_late)
         weigh_a(3, gt_late)
         project_b(2)
         project_b(3)
-        gi_table = repeat_gate(sbuf("gi_table", [P, CHUNK], F32)[:], gi_loaded)
+        gi_table = sbuf("gi_table", [P, CHUNK], F32)[:]
+        gpsimd_round(
+            gi_table.rearrange("p (m t) -> p m t", t=PACK), gi_loaded[:].unsqueeze(1).to_broadcast([P, SHARE, PACK])
+        )
         weigh_b(0, gi_table)
-        pairs = {c: weigh_b_in_pairs(c, gi_table) for c in PAIRED}
+        pairs = {c: weigh_b_in_pairs(c, gi_loaded) for c in PAIRED}
         z_mx = quantize_z(0, RAW_BYTES)
         first = quantize_z2(0)
         weave(1, pairs[1])
-        z_mx = z_mx + quantize_z(1, "picked_scale")
+        z_mx = z_mx + quantize_z(1, "wb_early")
         pool_first_chunk(z_mx, first)
         pool_chunk(1, z_mx, quantize_z2(1))
         weigh_b(3, gi_table)
@@ -292,8 +299,7 @@ def tile_picked_bilpool_relu_po_kernel(
                 in_=y_bf[:, first * PACK : last * PACK],
             )
 
-        round_y(0)
-        round_y(1)
+        round_rows(nc.vector.tensor_copy, y_bf[:, cols(0, HALF * PACK)], y_early[:])
         nc.vector.tensor_scalar(
             y_bf[:, cols(2, CHUNK * PACK)].rearrange("p (n t) -> p n t", t=PACK),
             y_again[:].rearrange("p t n -> p n t"),

@@ -162,8 +162,8 @@ def tile_picked_bilpool_relu_po_kernel(
         def round_wb_on_gpsimd(c):
             gpsimd_round(wb_bf[c][:].rearrange("p (n j) -> p n j", j=PACK), wb_raw[c].rearrange("p j n -> p n j"))
 
-        def round_wa_on_gpsimd(c):
-            gpsimd_round(
+        def round_wa_on_vector(c):
+            nc.vector.tensor_copy(
                 wa_bf[c][:].rearrange("p (u m j) -> p m u j", u=PACK, j=PACK),
                 wa_raw[c].rearrange("p j (m u) -> p m u j", u=PACK),
             )
@@ -247,7 +247,7 @@ def tile_picked_bilpool_relu_po_kernel(
         gt_early = repeat_gate(wa_raw[2][:, 0, :], gt_loaded)
         project_a(0)
         project_a(1)
-        round_wa_on_gpsimd(3)
+        round_wa_on_vector(3)
         round_wb(0, nc.scalar.copy)
         round_wb_on_gpsimd(1)
         gt_late = repeat_gate(at(0, "gt_late", [P, CHUNK], F32)[:], gt_loaded)
@@ -264,12 +264,9 @@ def tile_picked_bilpool_relu_po_kernel(
         weigh_a(3, gt_late)
         project_b(2)
         project_b(3)
-        gi_table = sbuf("gi_table", [P, CHUNK], F32)[:]
-        gpsimd_round(
-            gi_table.rearrange("p (m t) -> p m t", t=PACK), gi_loaded[:].unsqueeze(1).to_broadcast([P, SHARE, PACK])
-        )
+        gi_table = repeat_gate(sbuf("gi_table", [P, CHUNK], F32)[:], gi_loaded)
         weigh_b(0, gi_table)
-        pairs = {c: weigh_b_in_pairs(c, gi_loaded) for c in PAIRED}
+        pairs = {c: weigh_b_in_pairs(c, gi_table) for c in PAIRED}
         z_mx = quantize_z(0, RAW_BYTES)
         first = quantize_z2(0)
         weave(1, pairs[1])

@@ -259,7 +259,11 @@ def tile_picked_bilpool_relu_po_kernel(
         early = slices(*quantize("wb01", wb_early[:], HALF), 2)
         product(b_banks[1], x_mx, early[1])
         product(b_banks[0], x_mx, early[0])
-        round_wb_on_gpsimd(3)
+        round_rows(nc.scalar.copy, wb_bf[3][:, : SHARE * PACK], wb_raw[3][:, :, :SHARE])
+        gpsimd_round(
+            wb_bf[3][:, SHARE * PACK :].rearrange("p (n j) -> p n j", j=PACK),
+            wb_raw[3][:, :, SHARE:].rearrange("p j n -> p n j"),
+        )
         weigh_a(2, gt_late)
         weigh_a(3, gt_late)
         project_b(2)

from contextlib import ExitStack

import concourse.mybir as mybir

K, T, S, H = 512, 2048, 512, 512
FLOPS = 2 * K * S * H + 2 * K * S * H + 2 * S * H * H

F32 = mybir.dt.float32
BF16 = mybir.dt.bfloat16
I32 = mybir.dt.int32
U32 = mybir.dt.uint32
U16 = mybir.dt.uint16
U8 = mybir.dt.uint8
FP8X4 = mybir.dt.float8_e4m3fn_x4
ALU = mybir.AluOpType
COPY = mybir.ActivationFunctionType.Copy

P = 128
PACK = 4
QUADRANT = 32
BLOCK = 8
CHUNK = 128
CHUNKS = H // CHUNK
HALF = H // 2
SHARE = CHUNK // PACK
RUN = 8
OUT_SCALE = 0.0625
LEAD = T // 4
PAIRED = (1, 2)
RAW_BYTES = PACK * HALF * 4


def tile_picked_bilpool_relu_po_kernel(
    tc, x_words, x_scales, wa, wb, gt, gi, offs, out_0, out_1, out_2
):
    nc = tc.nc
    with ExitStack() as ctx:
        keep = ctx.enter_context(tc.tile_pool(name="keep", bufs=1))
        placed = ctx.enter_context(tc.tile_pool(name="placed", bufs=1))
        psum = ctx.enter_context(tc.psum_pool(name="psum", bufs=1))

        def sbuf(name, shape, dtype, tag=""):
            return keep.tile(shape, dtype, name=name, tag=tag or name, align_bytes=64)

        def raw_half(name):
            return sbuf(name, [P, PACK, HALF], F32)

        def at(offset, name, shape, dtype):
            return placed.tile(shape, dtype, name=name, offset=offset, align_bytes=64)

        def bank(name, tag):
            return psum.tile([P, PACK, CHUNK], F32, name=name, tag=tag)

        def cols(c, width=CHUNK):
            return slice(c * width, (c + 1) * width)

        def load_gate(name, gate, tag=""):
            loaded = sbuf(name, [P, PACK], F32, tag)
            nc.sync.dma_start(loaded[:], gate.rearrange("(p t) o -> p (t o)", t=PACK))
            return loaded

        def repeat_gate(place, loaded):
            nc.scalar.copy(
                place.rearrange("p (m t) -> p m t", t=PACK), loaded[:].unsqueeze(1).to_broadcast([P, SHARE, PACK])
            )
            return place

        def by_columns(table):
            return table.rearrange("p (m t) -> p m t", t=PACK).unsqueeze(1).to_broadcast([P, PACK, SHARE, PACK])

        def load_half(raw, w, h):
            nc.sync.dma_start(raw[:], w.rearrange("(p j) c -> p j c", j=PACK)[:, :, cols(h, HALF)])
            return [raw[:, :, cols(i)] for i in range(HALF // CHUNK)]

        def round_rows(copy, rounded, rows):
            copy(
                rounded.rearrange("p (g i j) -> p g j i", i=RUN, j=PACK),
                rows.rearrange("p j (g i) -> p g j i", i=RUN),
            )

        def quantize(name, rounded, width, tag=""):
            if isinstance(tag, int):
                codes = at(tag, name + "_codes", [P, width], U32)
            else:
                codes = sbuf(name + "_codes", [P, width], U32, tag)
            scales = sbuf(name + "_scales", [P, width], U8)
            nc.vector.quantize_mx(out=codes[:].bitcast(FP8X4), scales=scales[:], in_=rounded)
            return codes, scales

        def slices(codes, scales, count):
            return [(codes[:, cols(t, P)], scales[:, cols(t, P)]) for t in range(count)]

        def product(acc, dealt, moving):
            for t, (codes, scales) in enumerate(dealt):
                nc.tensor.matmul_mx(
                    out=acc[:, t, :],
                    lhsT=codes.bitcast(FP8X4),
                    lhsT_scale=scales,
                    rhs=moving[0][:].bitcast(FP8X4),
                    rhs_scale=moving[1][:],
                    start=True,
                    stop=True,
                )

        word_table = sbuf("word_table", [P, T], I32)
        word_rows = x_words[0].rearrange("p n t -> p (n t)").bitcast(I32)
        nc.sync.dma_start(word_table[:, :LEAD], word_rows[:, :LEAD])
        offsets = keep.tile([P, S // 16], U16, name="offsets")
        nc.sync.dma_start(offsets[:], offs)

        scale_table = at(RAW_BYTES - T // 2, "scale_table", [P, T], U8)
        nc.vector.memset(scale_table[:].bitcast(I32), 0)
        x_scale = sbuf("x_scale", [P, S], U8)
        nc.vector.memset(x_scale[:].bitcast(I32), 0)
        nc.sync.dma_start(scale_table[0:P:BLOCK, :].bitcast(I32), x_scales[0].bitcast(I32))

        nc.sync.dma_start(word_table[:, LEAD:], word_rows[:, LEAD:])
        wa_raw = load_half(raw_half("wa_raw0"), wa, 0)
        wa_raw = wa_raw + load_half(raw_half("wa_raw1"), wa, 1)
        gt_loaded = load_gate("gt_loaded", gt)

        picked_scale = sbuf("picked_scale", [P, S], U8)
        nc.vector.tensor_copy(
            picked_scale[:].rearrange("p (t m) -> p m t", t=PACK), scale_table[:].indirect(offsets[:])
        )
        for r in range(PACK):
            nc.sync.dma_start(
                x_scale[r:P:QUADRANT, :].bitcast(I32), picked_scale[BLOCK * r : P : QUADRANT, :].bitcast(I32)
            )
        wb_raw = load_half(at(0, "wb_raw0", [P, PACK, HALF], F32), wb, 0)
        wb_raw = wb_raw + load_half(at(RAW_BYTES, "wb_raw1", [P, PACK, HALF], F32), wb, 1)
        gi_loaded = load_gate("gi_loaded", gi, "picked_scale")

        x_codes = sbuf("x_codes", [P, S], U32)
        nc.vector.tensor_copy(
            x_codes[:].rearrange("p (t m) -> p m t", t=PACK),
            word_table[:].bitcast(U32).indirect(offsets[:]),
        )
        x_mx = slices(x_codes, x_scale, PACK)
        z2_tags = ("z2_bf0", "z2_bf1", "z2_bf2", "pairs1")
        wa_tags = ("wa_bf0", "wa_bf1", "wa_bf2", "wa_bf0")

        wa_bf = [sbuf(f"wa_bf{c}", [P, CHUNK * PACK], BF16, wa_tags[c]) for c in range(CHUNKS)]
        wb_early = sbuf("wb_early", [P, HALF * PACK], BF16)
        wb_bf = [wb_early[:, cols(c, CHUNK * PACK)] for c in range(2)]
        wb_bf = wb_bf + [sbuf("wb_bf2", [P, CHUNK * PACK], BF16), sbuf("wb_bf3", [P, CHUNK * PACK], BF16, "wb_early")]
        a_banks = [bank(f"a{c}", f"first{c}") for c in range(CHUNKS)]
        b_banks = [bank(f"b{c}", f"second{c}") for c in range(CHUNKS)]

        def round_wa(c, copy):
            copy(
                wa_bf[c][:].rearrange("p (u m j) -> p m j u", u=PACK, j=PACK),
                wa_raw[c].rearrange("p j (m u) -> p m j u", u=PACK),
            )

        def round_wb(c, copy):
            round_rows(copy, wb_bf[c][:], wb_raw[c])

        def gpsimd_round(rounded, rows):
            nc.gpsimd.tensor_scalar(rounded, rows, 1.0, 0.0, ALU.mult, ALU.add)

        def round_wb_on_gpsimd(c):
            gpsimd_round(wb_bf[c][:].rearrange("p (n j) -> p n j", j=PACK), wb_raw[c].rearrange("p j n -> p n j"))

        def round_wa_on_vector(c):
            nc.vector.tensor_copy(
                wa_bf[c][:].rearrange("p (u m j) -> p m u j", u=PACK, j=PACK),
                wa_raw[c].rearrange("p j (m u) -> p m u j", u=PACK),
            )

        def project_a(c, tag=""):
            product(a_banks[c], x_mx, quantize(f"wa{c}", wa_bf[c][:], CHUNK, tag))

        def project_b(c, tag=""):
            product(b_banks[c], x_mx, quantize(f"wb{c}", wb_bf[c][:], CHUNK, tag))

        z_bf = sbuf("z_bf", [P, H * PACK], BF16)
        z_view = z_bf[:].rearrange("p (u c m t) -> p u c m t", u=PACK, c=CHUNKS, t=PACK)

        def weigh_a(c, table):
            nc.vector.scalar_tensor_tensor(
                out=z_view[:, :, c, :, :],
                in0=a_banks[c][:].rearrange("p t (u m) -> p u m t", u=PACK),
                scalar=0.0,
                in1=by_columns(table),
                op0=ALU.max,
                op1=ALU.mult,
            )

        pair_planes = {c: sbuf(f"pairs{c}", [P, 2, CHUNK, 2], BF16) for c in PAIRED}
        def quantize_z(h, tag):
            return slices(*quantize(f"z{h}", z_bf[:, cols(h, HALF * PACK)], HALF, tag), PACK // 2)

        z2_bf = [sbuf(f"z2_bf{c}", [P, CHUNK * PACK], BF16, z2_tags[c]) for c in range(CHUNKS)]

        def weigh_b(c, table):
            nc.vector.tensor_tensor(
                out=z2_bf[c][:].rearrange("p (u m t) -> p u m t", u=PACK, t=PACK),
                in0=b_banks[c][:].rearrange("p t (u m) -> p u m t", u=PACK),
                in1=by_columns(table),
                op=ALU.mult,
            )

        def weigh_b_on_scalar(c, table):
            for t in range(PACK):
                nc.scalar.activation(z2_bf[c][:, t::PACK], b_banks[c][:, t, :], COPY, scale=table[:, t : t + 1])

        def weigh_b_in_pairs(c, table):
            pairs = pair_planes[c]
            for t in (0, 2, 1, 3):
                nc.scalar.activation(
                    pairs[:, t // 2, :, t % 2], b_banks[c][:, t, :], COPY, scale=table[:, t : t + 1]
                )
            return pairs

        def weave(c, pairs):
            nc.vector.tensor_copy(
                z2_bf[c][:].bitcast(I32).rearrange("p (n u) -> p n u", u=2),
                pairs[:].rearrange("p u n e -> p (u n e)").bitcast(I32).rearrange("p (u n) -> p n u", u=2),
            )

        out_rows = out_0.rearrange("(p t) n -> p t n", t=PACK)
        y_early = sbuf("y_early", [P, PACK, HALF], F32)
        y_f32 = [y_early[:, :, cols(c)] for c in range(2)]
        y_f32 = y_f32 + [sbuf(f"y_f32_{c}", [P, PACK, CHUNK], F32) for c in range(2, CHUNKS)]

        def quantize_z2(c):
            return quantize(f"z2_{c}", z2_bf[c][:], CHUNK)

        def pool_first_chunk(z_mx, moving):
            for h, tag in enumerate(("first0", "second1")):
                rows = cols(h, PACK // 2)
                acc = psum.tile([P, PACK // 2, CHUNK], F32, name=f"y0_{h}", tag=tag)
                product(acc, z_mx[rows], moving)
                nc.scalar.activation(y_f32[0][:, rows, :], acc[:], COPY, scale=OUT_SCALE)
            nc.sync.dma_start(out_rows[:, :, cols(0)], y_f32[0][:])

        def pool_chunk(c, z_mx, moving):
            acc = bank(f"y{c}", f"first{c}")
            product(acc, z_mx, moving)
            nc.scalar.activation(y_f32[c][:], acc[:], COPY, scale=OUT_SCALE)
            nc.sync.dma_start(out_rows[:, :, cols(c)], y_f32[c][:])

        round_wa(0, nc.scalar.copy)
        round_wa(1, nc.scalar.copy)
        round_wa(2, nc.scalar.copy)
        gt_early = repeat_gate(wa_raw[2][:, 0, :], gt_loaded)
        project_a(0)
        project_a(1)
        round_wa_on_vector(3)
        round_wb(0, nc.scalar.copy)
        round_wb_on_gpsimd(1)
        gt_late = repeat_gate(at(0, "gt_late", [P, CHUNK], F32)[:], gt_loaded)
        round_wb(2, nc.scalar.copy)
        project_a(2)
        project_a(3)
        weigh_a(0, gt_early)
        weigh_a(1, gt_early)
        early = slices(*quantize("wb01", wb_early[:], HALF), 2)
        product(b_banks[1], x_mx, early[1])
        product(b_banks[0], x_mx, early[0])
        round_rows(nc.scalar.copy, wb_bf[3][:, : SHARE * PACK], wb_raw[3][:, :, :SHARE])
        gpsimd_round(
            wb_bf[3][:, SHARE * PACK :].rearrange("p (n j) -> p n j", j=PACK),
            wb_raw[3][:, :, SHARE:].rearrange("p j n -> p n j"),
        )
        weigh_a(2, gt_late)
        weigh_a(3, gt_late)
        project_b(2)
        project_b(3)
        gi_table = repeat_gate(sbuf("gi_table", [P, CHUNK], F32)[:], gi_loaded)
        weigh_b(0, gi_table)
        pairs = {c: weigh_b_in_pairs(c, gi_table) for c in PAIRED}
        z_mx = quantize_z(0, RAW_BYTES)
        first = quantize_z2(0)
        weave(1, pairs[1])
        z_mx = z_mx + quantize_z(1, "wb_early")
        pool_first_chunk(z_mx, first)
        pool_chunk(1, z_mx, quantize_z2(1))
        weigh_b(3, gi_table)
        weave(2, pairs[2])
        pool_chunk(3, z_mx, quantize_z2(3))
        last = quantize_z2(2)
        y_again = bank("y_again", "second0")
        product(y_again, z_mx, last)
        pool_chunk(2, z_mx, last)

        y_bf = sbuf("y_bf", [P, H * PACK], BF16, "pairs1")
        y_codes = sbuf("y_codes", [P, H], U32)
        y_scales = sbuf("y_scales", [P, H], U8)
        code_rows = out_1[0].rearrange("p n t -> p (n t)").bitcast(I32)

        def round_y(c):
            round_rows(nc.vector.tensor_copy, y_bf[:, cols(c, CHUNK * PACK)], y_f32[c][:])

        def quantize_y(first, last):
            nc.vector.quantize_mx(
                out=y_codes[:, first:last].bitcast(FP8X4),
                scales=y_scales[:, first:last],
                in_=y_bf[:, first * PACK : last * PACK],
            )

        round_rows(nc.vector.tensor_copy, y_bf[:, cols(0, HALF * PACK)], y_early[:])
        nc.vector.tensor_scalar(
            y_bf[:, cols(2, CHUNK * PACK)].rearrange("p (n t) -> p n t", t=PACK),
            y_again[:].rearrange("p t n -> p n t"),
            OUT_SCALE,
            None,
            ALU.mult,
        )
        round_y(3)
        quantize_y(0, HALF)
        quantize_y(HALF, H)
        nc.sync.dma_start(code_rows, y_codes[:].bitcast(I32))
        scale_out = out_2[0].bitcast(I32)
        for q in range(P // QUADRANT):
            queue = nc.scalar if q % 2 else nc.sync
            queue.dma_start(
                scale_out[4 * q : 4 * q + 4, :], y_scales[QUADRANT * q : QUADRANT * q + 4, :].bitcast(I32)
            )
